import numpy as np
import ml_dtypes


def mxq(x, axis, fmt="e4m3"):
    dtype, down = {"e4m3": (ml_dtypes.float8_e4m3fn, 7), "e5m2": (ml_dtypes.float8_e5m2, 14)}[fmt]
    v = np.moveaxis(np.asarray(x, np.float32).astype(ml_dtypes.bfloat16).astype(np.float64), axis, -1)
    blocks = v.reshape(v.shape[:-1] + (-1, 32))
    amax = np.abs(blocks).max(-1, keepdims=True)
    byte = np.maximum(np.where(amax > 0, np.frexp(amax)[1] - 1 + 127, 0) - down, 1)
    scale = np.exp2(byte - 127.0)
    codes = (blocks / scale).astype(np.float32).astype(dtype).astype(np.float64)
    return np.moveaxis((codes * scale).reshape(v.shape), -1, axis)


WIDE = False


def mx_kscale(k):
    if not WIDE:
        return np.ones(k)
    levels = np.array([10, -10, 5, -5, 0])
    if k % 512:
        return np.exp2(np.random.permutation(np.resize(levels, k // 32))).repeat(32)
    a = np.empty((k // 512, 16))
    for p in range(k // 512):
        a[p, :8] = np.random.permutation(np.resize(levels, 8))
        for g in range(8):
            far = levels[np.abs(levels - a[p, g]) >= 10]
            a[p, g + 8] = far[np.random.randint(len(far))]
    return np.exp2(a.ravel()).repeat(32)


BF16 = ml_dtypes.bfloat16


def bf(x):
    return np.asarray(x, np.float32).astype(BF16)


def f64(x):
    return np.asarray(x).astype(np.float64)


E2M1 = np.array([0.0, 0.5, 1.0, 1.5, 2.0, 3.0, 4.0, 6.0, -0.0, -0.5, -1.0, -1.5, -2.0, -3.0, -4.0, -6.0])


def pack_weight(w, fmt):
    k, n = w.shape
    w = f64(bf(w)).reshape(k // 32, 32, n)
    amax = np.abs(w).max(1)
    if fmt == "e4m3":
        byte = np.frexp(amax)[1] - 1 + 127 - 7
    else:
        mant, ex = np.frexp(amax / 6.0)
        byte = np.where(mant > 0.5, ex, ex - 1) + 127
    byte = np.clip(np.where(amax > 0, byte, 1), 1, 254)
    scaled = (w * np.exp2(127.0 - byte)[:, None, :]).reshape(k, n).astype(np.float32)
    by_word = np.ascontiguousarray(scaled.reshape(k // 512, 128, 4, n).transpose(0, 1, 3, 2))
    if fmt == "e4m3":
        words = by_word.astype(ml_dtypes.float8_e4m3fn).view(np.uint8)
    else:
        c = by_word.astype(ml_dtypes.float4_e2m1fn).view(np.uint8) & 0xF
        words = c[..., 0::2] | (c[..., 1::2] << 4)
    return np.ascontiguousarray(words), np.ascontiguousarray(byte.astype(np.uint8).reshape(k // 512, 16, n))


def unpack_weight(words, scales, fmt):
    g, p, n, _ = words.shape
    if fmt == "e4m3":
        vals = np.ascontiguousarray(words).view(ml_dtypes.float8_e4m3fn).astype(np.float64)
    else:
        nib = np.empty((g, p, n, 4), np.uint8)
        nib[..., 0::2] = words & 0xF
        nib[..., 1::2] = words >> 4
        vals = E2M1[nib]
    vals = vals * np.repeat(np.exp2(scales.astype(np.float64) - 127.0), 8, axis=1)[..., None]
    return vals.transpose(0, 1, 3, 2).reshape(g * 512, n)
def pack4(w):
    words, scales = pack_weight(w, "e2m1")
    return words.reshape(words.shape[0], 128, -1), scales


def unpack4(words, scales):
    return unpack_weight(words.reshape(words.shape[0], 128, -1, 2), scales, "e2m1")


E4M3FN = np.array([(-1.0 if i & 128 else 1.0) * ((1.0 + (i & 7) / 8.0) * 2.0 ** (((i >> 3) & 15) - 7) if i & 120 else (i & 7) * 2.0 ** -9) for i in range(256)])


def e4m3fn_bytes(y):
    return np.clip(np.asarray(y, np.float64), -448.0, 448.0).astype(np.float32).astype(ml_dtypes.float8_e4m3fn).view(np.uint8)


def e4m3fn_values(b):
    return E4M3FN[b]


T, K, N, R, B = 1024, 2048, 1024, 1024, 128


def setup_inputs():
    s, t = mx_kscale(K), mx_kscale(N)
    h = np.random.standard_normal((T, K)) * s
    h_scale = (np.abs(h.reshape(T, K // B, B)).max(axis=2) / 448.0).astype(np.float32)
    h_bytes = e4m3fn_bytes(h / np.repeat(f64(h_scale), B, axis=1))
    w = np.random.standard_normal((N, R)) / np.sqrt(N) / t[:, None]
    w_words, w_scales = pack4(w)
    return {"H_bytes": h_bytes,
            "H_scale": h_scale,
            "C": bf(np.random.standard_normal((K, N)) / np.sqrt(K) / s[:, None] * t),
            "u": bf(np.random.standard_normal((T, N))),
            "d": bf(np.random.standard_normal(N) * t),
            "W_words": w_words,
            "W_scales": w_scales,
            "gate": bf(np.random.standard_normal((T, R)))}


def reference(H_bytes, H_scale, C, u, d, W_words, W_scales, gate):
    H = e4m3fn_values(H_bytes) * np.repeat(f64(H_scale), B, axis=1)
    y = mxq(H, 1, "e4m3") @ mxq(f64(C), 0, "e4m3")
    y = y + f64(d) * f64(u)
    o = mxq(y, 1, "e4m3") @ unpack4(W_words, W_scales)
    return o * (1.0 / (1.0 + np.exp(-f64(gate))))

@@ -1,0 +1,304 @@
+from contextlib import ExitStack
+
+import concourse.mybir as mybir
+from concourse.masks import make_identity
+
+T, K, N, R = 1024, 2048, 1024, 1024
+FLOPS = 2 * T * K * N + 2 * T * N * R
+
+F32 = mybir.dt.float32
+BF16 = mybir.dt.bfloat16
+U8 = mybir.dt.uint8
+U32 = mybir.dt.uint32
+I32 = mybir.dt.int32
+FP8 = mybir.dt.float8_e4m3fn
+FP8X4 = mybir.dt.float8_e4m3fn_x4
+FP4X4 = mybir.dt.float4_e2m1fn_x4
+ACT = mybir.ActivationFunctionType
+ALU = mybir.AluOpType
+
+P = 128
+TILES = T // P
+PASS = 512
+H_PASSES = K // PASS
+Y_PASSES = N // PASS
+HALVES = 2
+HALF = 512
+BLOCK = 128
+BLOCKS = K // BLOCK
+GATE_HEAD = 64
+TEMPLATE = [('m1', 0, 24), ('du', 0, 2), ('hq', 0, 3), ('om', 1, -4), ('hq', 1, 3), ('m2', 1, -3), ('th', 0, 4), ('du', 1, 2), ('yo', 0, -1), ('cq', 1, 4), ('th', 1, 4), ('ci', 1, 5), ('ya', 0, 1), ('w', 1, 5), ('om', 0, -4), ('ty', 0, 0), ('w', 3, 5), ('ho', 0, 4), ('ho', 1, 4), ('w', 2, 5), ('m2', 0, -3), ('ci', 0, 7), ('yq', 0, -1), ('sg', 0, -2), ('m1', 1, 24), ('ya', 1, 1), ('w', 0, 6), ('cq', 0, 6)]
+ENG = {'ph': 4, 'k': 3, 'gap': 3, ('w', 0, 0): 'S', ('w', 1, 0): 'V', ('w', 2, 0): 'V', ('w', 3, 0): 'V', ('ho', 0, 0): 'S', ('du', 0, 0): 'V', ('ho', 1, 0): 'S', ('du', 1, 0): 'V', ('yo', 0, 0): 'S', ('w', 0, 1): 'S', ('w', 1, 1): 'S', ('w', 2, 1): 'V', ('w', 3, 1): 'S', ('ho', 0, 1): 'S', ('du', 0, 1): 'V', ('ho', 1, 1): 'S', ('du', 1, 1): 'V', ('yo', 0, 1): 'S', ('ci', 0, 0): 'V', ('ci', 0, 1): 'S', ('ci', 0, 2): 'V', ('ci', 0, 3): 'V', ('ci', 1, 0): 'V', ('ci', 1, 1): 'S', ('ci', 1, 2): 'S', ('ci', 1, 3): 'S'}
+D_STEP = -6
+LOADS = ['Hs',('H',0),'gh',('H',1),('C',0),'d',('H',2),('C',1),('C',2),('H',3),('C',3),('u',0),('u',1),('H',4),'W',('g',0),('u',2),('g',1),('H',5),('u',3),('g',2),('H',6),('u',4),('g',3),('H',7),('u',5),('g',4),('u',6),('g',5),('u',7),('g',6),('g',7)]
+
+
+def tile_state_space_readout_d4_kernel(tc, H_bytes, H_scale, C, u, d, W_words, W_scales, gate, out):
+    nc = tc.nc
+    h_rows = H_bytes.rearrange("(p i) k -> p i k", i=TILES)
+    u_rows = u.rearrange("(p i) n -> p i n", i=TILES)
+    gate_rows = gate.rearrange("(p i) n -> p i n", i=TILES)
+    out_rows = out.rearrange("(p i) n -> p i n", i=TILES)
+
+    with ExitStack() as ctx:
+        keep = ctx.enter_context(tc.tile_pool(name="keep", bufs=1))
+        work = ctx.enter_context(tc.tile_pool(name="work", bufs=2))
+        psum = ctx.enter_context(tc.psum_pool(name="psum", bufs=1))
+        ctx.enter_context(tc.manual_schedule())
+
+        free_banks = list(range(8))
+        held = {}
+
+        def bank(key, shape, dtype=F32):
+            held[key] = free_banks.pop(0)
+            return psum.tile(shape, dtype, name=f"bank{held[key]}")
+
+        def release(key):
+            free_banks.append(held[key])
+
+        ident = keep.tile([P, P], F32, name="ident")
+        ones = keep.tile([P, P], BF16, name="ones")
+        d_row = keep.tile([P, N], BF16, name="d_row")
+        d_all = keep.tile([P, N], BF16, name="d_all")
+        h_scale = keep.tile([P, TILES, BLOCKS], F32, name="h_scale")
+        h_bytes = keep.tile([P, TILES, K], U8, name="h_bytes")
+        c_raw = keep.tile([P, H_PASSES, 4, N], BF16, name="c_raw")
+        u_sb = keep.tile([P, TILES, N], BF16, name="u_sb")
+        gate_sb = keep.tile([P, TILES, R], BF16, name="gate_sb")
+        w_words = keep.tile([P, Y_PASSES, 2 * R], U8, name="w_words", align_bytes=256)
+        w_scales = keep.tile([P, Y_PASSES, R], U8, name="w_scales", align_bytes=256)
+        c_codes = keep.tile([P, H_PASSES, N], U32, name="c_codes", align_bytes=256)
+        c_scales = keep.tile([P, H_PASSES, N], U8, name="c_scales", align_bytes=256)
+        h_codes = keep.tile([P, TILES, H_PASSES * P], U32, name="h_codes", align_bytes=256)
+        h_scales = keep.tile([P, TILES, H_PASSES * P], U8, name="h_scales", align_bytes=256)
+
+        make_identity(nc, ident[:])
+        nc.vector.memset(d_row[:].bitcast(I32), 0)
+        nc.vector.memset(ones[:], 1.0)
+        nc.gpsimd.memset(w_scales[:].rearrange("p g n -> p (g n)").bitcast(I32), 0)
+
+        def load_rows(dst, src, i0, i1):
+            nc.sync.dma_start(out=dst[:, i0:i1, :], in_=src[:, i0:i1, :])
+
+        for item in LOADS:
+            if item == "Hs":
+                nc.sync.dma_start(out=h_scale[:], in_=H_scale.rearrange("(p i) j -> p i j", i=TILES))
+            elif item == "gh":
+                nc.sync.dma_start(out=gate_sb[:, 0, :GATE_HEAD], in_=gate_rows[:, 0, :GATE_HEAD])
+            elif item == "d":
+                nc.sync.dma_start(out=d_row[0:1, :], in_=d.rearrange("(o n) -> o n", o=1))
+            elif item == "W":
+                for q in range(4):
+                    nc.sync.dma_start(
+                        out=w_scales[32 * q : 32 * q + 4, :, :].bitcast(I32),
+                        in_=W_scales[:, 4 * q : 4 * q + 4, :].rearrange("g r n -> r g n").bitcast(I32),
+                    )
+                nc.sync.dma_start(out=w_words[:].bitcast(I32), in_=W_words.rearrange("g p b -> p g b").bitcast(I32))
+            elif item[0] == "C":
+                g = item[1]
+                nc.sync.dma_start(out=c_raw[:, g, :, :], in_=C[g * PASS : (g + 1) * PASS, :].rearrange("(p j) n -> p j n", j=4))
+            elif item == ("g", 0):
+                nc.sync.dma_start(out=gate_sb[:, 0, GATE_HEAD:], in_=gate_rows[:, 0, GATE_HEAD:])
+            else:
+                dst, src = {"H": (h_bytes, h_rows), "u": (u_sb, u_rows), "g": (gate_sb, gate_rows)}[item[0]]
+                load_rows(dst, src, item[1], item[1] + 1)
+
+        sig = {}
+        h_wide, h_banks, h_turned, c_grouped = {}, {}, {}, {}
+        y_banks, skip, y_sb, y_bank, y_turned, y_codes, y_scales, o_banks = {}, {}, {}, {}, {}, {}, {}, {}
+
+        def widen(i, blocks, on_vector):
+            if i not in h_wide:
+                h_wide[i] = work.tile([P, K], BF16, name="h_wide", bufs=4)
+            for j in blocks:
+                cols = slice(j * BLOCK, (j + 1) * BLOCK)
+                src = h_bytes[:, i, cols].bitcast(FP8)
+                scale = h_scale[:, i, j : j + 1]
+                if on_vector:
+                    nc.vector.tensor_scalar(out=h_wide[i][:, cols], in0=src, scalar1=scale, scalar2=None, op0=ALU.mult)
+                else:
+                    nc.scalar.activation(out=h_wide[i][:, cols], in_=src, func=ACT.Copy, scale=scale)
+
+        def turn_h(i, b):
+            words = h_wide[i][:].bitcast(F32)
+            h_banks[i, b] = bank(("h", i, b), [P, 2, 2, P])
+            for gg in range(2):
+                g = 2 * b + gg
+                for w in range(2):
+                    nc.tensor.transpose(h_banks[i, b][:, gg, w, :], words[:, 256 * g + w : 256 * (g + 1) : 2], ident[:])
+
+        def empty_h(i, b, e):
+            h_turned[i, b] = work.tile([P, 2 * P * 4], BF16, name="h_turned", bufs=4, align_bytes=256)
+            dst = h_turned[i, b][:].bitcast(F32).rearrange("p (g t w) -> p g t w", g=2, w=2)
+            src = h_banks[i, b][:].rearrange("p g w t -> p g t w")
+            if e == "V":
+                nc.vector.tensor_copy(out=dst, in_=src)
+            else:
+                nc.scalar.copy(out=dst, in_=src)
+            release(("h", i, b))
+
+        def quantize_h(i, b):
+            cols = slice(2 * b * P, 2 * (b + 1) * P)
+            nc.vector.quantize_mx(out=h_codes[:, i, cols].bitcast(FP8X4), scales=h_scales[:, i, cols], in_=h_turned[i, b][:])
+
+        def group_c(g, h, e):
+            c_grouped[g, h] = work.tile([P, HALF * 4], BF16, name="c_grouped", bufs=4, align_bytes=256)
+            dst = c_grouped[g, h][:].rearrange("p (w m e j) -> p m j w e", w=2, e=2, j=4)
+            src = c_raw[:, g, :, h * HALF : (h + 1) * HALF].rearrange("p j (m w e) -> p m j w e", w=2, e=2)
+            if e == "V":
+                nc.vector.tensor_copy(out=dst, in_=src)
+            else:
+                nc.scalar.copy(out=dst, in_=src)
+
+        def quantize_c(g, h):
+            cols = slice(h * HALF, (h + 1) * HALF)
+            nc.vector.quantize_mx(out=c_codes[:, g, cols].bitcast(FP8X4), scales=c_scales[:, g, cols], in_=c_grouped[g, h][:])
+
+        def readout(i, h, g):
+            if g == 0:
+                y_banks[i, h] = bank(("y", i, h), [P, HALF])
+            tok = slice(g * P, (g + 1) * P)
+            cols = slice(h * HALF, (h + 1) * HALF)
+            nc.tensor.matmul_mx(
+                out=y_banks[i, h][:],
+                lhsT=h_codes[:, i, tok].bitcast(FP8X4),
+                lhsT_scale=h_scales[:, i, tok],
+                rhs=c_codes[:, g, cols].bitcast(FP8X4),
+                rhs_scale=c_scales[:, g, cols],
+                start=(g == 0),
+                stop=(g == H_PASSES - 1),
+            )
+
+        def spread_d():
+            acc = bank("d", [P, N], BF16)
+            for h in range(HALVES):
+                cols = slice(h * HALF, (h + 1) * HALF)
+                nc.tensor.matmul(acc[:, cols], lhsT=ones[:], rhs=d_row[:, cols], start=True, stop=True)
+            nc.scalar.copy(out=d_all[:], in_=acc[:])
+            release("d")
+
+        def skip_term(i, h, e):
+            cols = slice(h * HALF, (h + 1) * HALF)
+            skip[i, h] = work.tile([P, HALF], F32, name="skip", bufs=4)
+            eng = nc.gpsimd if e == "G" else nc.vector
+            eng.tensor_tensor(out=skip[i, h][:], in0=u_sb[:, i, cols], in1=d_all[:, cols], op=ALU.mult)
+
+        def add_skip(i, h):
+            if i not in y_sb:
+                y_sb[i] = work.tile([P, N], BF16, name="y_sb", bufs=4)
+            nc.vector.tensor_tensor(
+                out=y_sb[i][:, h * HALF : (h + 1) * HALF].rearrange("p (w m e) -> p w m e", w=2, e=2),
+                in0=y_banks[i, h][:].rearrange("p (w m e) -> p w m e", w=2, e=2),
+                in1=skip[i, h][:].rearrange("p (m w e) -> p w m e", w=2, e=2),
+                op=ALU.add,
+            )
+            release(("y", i, h))
+
+        def turn_y(i):
+            words = y_sb[i][:].bitcast(F32)
+            y_bank[i] = bank(("t", i), [P, 2, 2, P])
+            for g in range(Y_PASSES):
+                for w in range(2):
+                    c0 = 256 * g + P * w
+                    nc.tensor.transpose(y_bank[i][:, g, w, :], words[:, c0 : c0 + P], ident[:])
+
+        def empty_y(i, e):
+            y_turned[i] = work.tile([P, 2 * P * 4], BF16, name="y_turned", align_bytes=256)
+            dst = y_turned[i][:].bitcast(F32).rearrange("p (g t w) -> p g t w", g=2, w=2)
+            src = y_bank[i][:].rearrange("p g w t -> p g t w")
+            if e == "V":
+                nc.vector.tensor_copy(out=dst, in_=src)
+            else:
+                nc.scalar.copy(out=dst, in_=src)
+            release(("t", i))
+
+        def quantize_y(i):
+            y_codes[i] = work.tile([P, Y_PASSES * P], U32, name="y_codes", bufs=3, align_bytes=256)
+            y_scales[i] = work.tile([P, Y_PASSES * P], U8, name="y_scales", bufs=3, align_bytes=256)
+            nc.vector.quantize_mx(out=y_codes[i][:].bitcast(FP8X4), scales=y_scales[i][:], in_=y_turned[i][:])
+
+        def project(i, h):
+            o_banks[i, h] = bank(("o", i, h), [P, HALF])
+            for g in range(Y_PASSES):
+                tok = slice(g * P, (g + 1) * P)
+                nc.tensor.matmul_mx(
+                    out=o_banks[i, h][:],
+                    lhsT=y_codes[i][:, tok].bitcast(FP8X4),
+                    lhsT_scale=y_scales[i][:, tok],
+                    rhs=w_words[:, g, 2 * h * HALF : 2 * (h + 1) * HALF].bitcast(FP4X4),
+                    rhs_scale=w_scales[:, g, h * HALF : (h + 1) * HALF],
+                    start=(g == 0),
+                    stop=(g == Y_PASSES - 1),
+                )
+
+        def squash(i, c0, c1):
+            if i not in sig:
+                sig[i] = work.tile([P, R], F32, name="sig", bufs=4)
+            nc.scalar.activation(out=sig[i][:, c0:c1], in_=gate_sb[:, i, c0:c1], func=ACT.Sigmoid)
+
+        def apply_gate(i, h):
+            o_sb = work.tile([P, HALF], F32, name="o_sb", bufs=8)
+            cols = slice(h * HALF, (h + 1) * HALF)
+            nc.vector.tensor_tensor(out=o_sb[:], in0=o_banks[i, h][:], in1=sig[i][:, cols], op=ALU.mult)
+            release(("o", i, h))
+            nc.sync.dma_start(out=out_rows[:, i, cols], in_=o_sb[:])
+
+        squash(0, 0, GATE_HEAD)
+        done = set()
+        for s in range(-9, 12):
+            if s == D_STEP:
+                spread_d()
+            for k, a, off in TEMPLATE:
+                i = s + off
+                if k in ("ci", "cq"):
+                    if 0 <= i < H_PASSES:
+                        if k == "ci":
+                            group_c(i, a, ENG["ci", a, i])
+                        else:
+                            quantize_c(i, a)
+                        done.add((k, i, a))
+                    continue
+                if k == "m1":
+                    for j in range(0, min(max(i, ENG["k"] - 1), TILES - 1) + 1):
+                        for g in range(H_PASSES):
+                            if ("m1", j, a, g) in done:
+                                continue
+                            if ("hq", j, g // 2) in done and ("cq", g, a) in done:
+                                readout(j, a, g)
+                                done.add(("m1", j, a, g))
+                            else:
+                                break
+                    continue
+                if k in ("w", "th", "ho", "hq"):
+                    if 0 <= i + ENG["gap"] < ENG["k"]:
+                        i += ENG["gap"]
+                    elif i < ENG["k"]:
+                        continue
+                if not 0 <= i < TILES:
+                    continue
+                ph = 0 if i < ENG["ph"] else 1
+                if k == "w":
+                    widen(i, range(4 * a, 4 * a + 4), ENG["w", a, ph] == "V")
+                elif k == "th":
+                    turn_h(i, a)
+                elif k == "ho":
+                    empty_h(i, a, ENG["ho", a, ph])
+                elif k == "hq":
+                    quantize_h(i, a)
+                    done.add((k, i, a))
+                elif k == "du":
+                    skip_term(i, a, ENG["du", a, ph])
+                elif k == "ya":
+                    add_skip(i, a)
+                elif k == "ty":
+                    turn_y(i)
+                elif k == "yo":
+                    empty_y(i, ENG["yo", 0, ph])
+                elif k == "yq":
+                    quantize_y(i)
+                elif k == "sg":
+                    squash(i, GATE_HEAD if i == 0 else 0, R)
+                elif k == "m2":
+                    project(i, a)
+                else:
+                    apply_gate(i, a)

@@ -27,10 +27,10 @@ HALF = 512
 BLOCK = 128
 BLOCKS = K // BLOCK
 GATE_HEAD = 64
-TEMPLATE = [('m1', 0, 24), ('du', 0, 2), ('hq', 0, 3), ('om', 1, -4), ('hq', 1, 3), ('m2', 1, -3), ('th', 0, 4), ('du', 1, 2), ('yo', 0, -1), ('cq', 1, 4), ('th', 1, 4), ('ci', 1, 5), ('ya', 0, 1), ('w', 1, 5), ('om', 0, -4), ('ty', 0, 0), ('w', 3, 5), ('ho', 0, 4), ('ho', 1, 4), ('w', 2, 5), ('m2', 0, -3), ('ci', 0, 7), ('yq', 0, -1), ('sg', 0, -2), ('m1', 1, 24), ('ya', 1, 1), ('w', 0, 6), ('cq', 0, 6)]
-ENG = {'ph': 4, 'k': 3, 'gap': 3, ('w', 0, 0): 'S', ('w', 1, 0): 'V', ('w', 2, 0): 'V', ('w', 3, 0): 'V', ('ho', 0, 0): 'S', ('du', 0, 0): 'V', ('ho', 1, 0): 'S', ('du', 1, 0): 'V', ('yo', 0, 0): 'S', ('w', 0, 1): 'S', ('w', 1, 1): 'S', ('w', 2, 1): 'V', ('w', 3, 1): 'S', ('ho', 0, 1): 'S', ('du', 0, 1): 'V', ('ho', 1, 1): 'S', ('du', 1, 1): 'V', ('yo', 0, 1): 'S', ('ci', 0, 0): 'V', ('ci', 0, 1): 'S', ('ci', 0, 2): 'V', ('ci', 0, 3): 'V', ('ci', 1, 0): 'V', ('ci', 1, 1): 'S', ('ci', 1, 2): 'S', ('ci', 1, 3): 'S'}
-D_STEP = -6
-LOADS = ['Hs',('H',0),'gh',('H',1),('C',0),'d',('H',2),('C',1),('C',2),('H',3),('C',3),('u',0),('u',1),('H',4),'W',('g',0),('u',2),('g',1),('H',5),('u',3),('g',2),('H',6),('u',4),('g',3),('H',7),('u',5),('g',4),('u',6),('g',5),('u',7),('g',6),('g',7)]
+TEMPLATE = [('m1', 1, 3), ('th', 0, 4), ('w', 1, 5), ('cq', 1, 5), ('hq', 0, 3), ('ty', 0, -1), ('ya', 0, 0), ('th', 1, 4), ('sg', 0, -3), ('m2', 0, -3), ('w', 3, 5), ('ya', 1, 1), ('m1', 0, 58), ('ci', 1, 6), ('om', 0, -4), ('om', 1, -4), ('hq', 1, 3), ('ho', 0, 4), ('cq', 0, 5), ('du', 1, 2), ('ci', 0, 6), ('w', 2, 5), ('ho', 1, 4), ('du', 0, 2), ('yo', 0, -1), ('w', 0, 6), ('yq', 0, -2), ('m2', 1, -3)]
+ENG = {'ph': 0, 'phd': 3, 'k': 3, 'gap': 3, ('w', 0, 0): 'S', ('w', 1, 0): 'V', ('w', 2, 0): 'V', ('w', 3, 0): 'V', ('ho', 0, 0): 'V', ('du', 0, 0): 'V', ('ho', 1, 0): 'S', ('du', 1, 0): 'V', ('yo', 0, 0): 'V', ('w', 0, 1): 'V', ('w', 1, 1): 'S', ('w', 2, 1): 'S', ('w', 3, 1): 'S', ('ho', 0, 1): 'S', ('du', 0, 1): 'V', ('ho', 1, 1): 'S', ('du', 1, 1): 'V', ('yo', 0, 1): 'S', ('ci', 0, 0): 'V', ('ci', 0, 1): 'S', ('ci', 0, 2): 'V', ('ci', 0, 3): 'S', ('ci', 1, 0): 'V', ('ci', 1, 1): 'V', ('ci', 1, 2): 'S', ('ci', 1, 3): 'V', ('co', 0, 0): 'S', ('co', 1, 0): 'V', ('W', 0, 0): 'V', ('W', 0, 1): 'S', ('W', 0, 2): 'V', ('W', 0, 3): 'S', ('W', 0, 4): 'S', ('W', 0, 5): 'S', ('W', 0, 6): 'S', ('W', 0, 7): 'S', ('W', 1, 0): 'S', ('W', 1, 1): 'V', ('W', 1, 2): 'V', ('W', 1, 3): 'S', ('W', 1, 4): 'S', ('W', 1, 5): 'S', ('W', 1, 6): 'S', ('W', 1, 7): 'S', ('W', 2, 0): 'V', ('W', 2, 1): 'V', ('W', 2, 2): 'S', ('W', 2, 3): 'S', ('W', 2, 4): 'V', ('W', 2, 5): 'S', ('W', 2, 6): 'V', ('W', 2, 7): 'S', ('W', 3, 0): 'V', ('W', 3, 1): 'V', ('W', 3, 2): 'S', ('W', 3, 3): 'V', ('W', 3, 4): 'S', ('W', 3, 5): 'S', ('W', 3, 6): 'S', ('W', 3, 7): 'S'}
+D_STEP = -7
+LOADS = ('Hs', ('H', 0), 'gh', 'd', ('H', 1), ('H', 2), ('C', 0), ('C', 1), ('C', 2), ('H', 3), ('C', 3), ('H', 4), ('u', 0), ('u', 1), ('H', 5), ('u', 2), ('H', 6), ('u', 3), ('H', 7), ('u', 4), ('u', 5), 'W', ('g', 0), ('g', 1), ('u', 6), ('g', 2), ('u', 7), ('g', 3), ('g', 4), ('g', 5), ('g', 6), ('g', 7))
 
 
 def tile_state_space_readout_d4_kernel(tc, H_bytes, H_scale, C, u, d, W_words, W_scales, gate, out):
@@ -86,7 +86,7 @@ def tile_state_space_readout_d4_kernel(tc, H_bytes, H_scale, C, u, d, W_words, W
             elif item == "gh":
                 nc.sync.dma_start(out=gate_sb[:, 0, :GATE_HEAD], in_=gate_rows[:, 0, :GATE_HEAD])
             elif item == "d":
-                nc.sync.dma_start(out=d_row[0:1, :], in_=d.rearrange("(o n) -> o n", o=1))
+                nc.scalar.dma_start(out=d_row[0:1, :], in_=d.rearrange("(o n) -> o n", o=1))
             elif item == "W":
                 for q in range(4):
                     nc.sync.dma_start(
@@ -276,9 +276,9 @@ def tile_state_space_readout_d4_kernel(tc, H_bytes, H_scale, C, u, d, W_words, W
                         continue
                 if not 0 <= i < TILES:
                     continue
-                ph = 0 if i < ENG["ph"] else 1
+                ph = 0 if i < ENG["phd" if k == "du" else "ph"] else 1
                 if k == "w":
-                    widen(i, range(4 * a, 4 * a + 4), ENG["w", a, ph] == "V")
+                    widen(i, range(4 * a, 4 * a + 4), ENG["W", a, i] == "V")
                 elif k == "th":
                     turn_h(i, a)
                 elif k == "ho":

@@ -19,18 +19,63 @@ ALU = mybir.AluOpType
 
 P = 128
 TILES = T // P
-PASS = 512
+PACK = 4
+PASS = P * PACK
+PAIRS = PASS // 2
 H_PASSES = K // PASS
 Y_PASSES = N // PASS
-HALVES = 2
 HALF = 512
-BLOCK = 128
-BLOCKS = K // BLOCK
-GATE_HEAD = 64
-TEMPLATE = [('m1', 1, 3), ('th', 0, 4), ('w', 1, 5), ('cq', 1, 5), ('hq', 0, 3), ('ty', 0, -1), ('ya', 0, 0), ('th', 1, 4), ('sg', 0, -3), ('m2', 0, -3), ('w', 3, 5), ('ya', 1, 1), ('m1', 0, 58), ('ci', 1, 6), ('om', 0, -4), ('om', 1, -4), ('hq', 1, 3), ('ho', 0, 4), ('cq', 0, 5), ('du', 1, 2), ('ci', 0, 6), ('w', 2, 5), ('ho', 1, 4), ('du', 0, 2), ('yo', 0, -1), ('w', 0, 6), ('yq', 0, -2), ('m2', 1, -3)]
-ENG = {'ph': 0, 'phd': 3, 'k': 3, 'gap': 3, ('w', 0, 0): 'S', ('w', 1, 0): 'V', ('w', 2, 0): 'V', ('w', 3, 0): 'V', ('ho', 0, 0): 'V', ('du', 0, 0): 'V', ('ho', 1, 0): 'S', ('du', 1, 0): 'V', ('yo', 0, 0): 'V', ('w', 0, 1): 'V', ('w', 1, 1): 'S', ('w', 2, 1): 'S', ('w', 3, 1): 'S', ('ho', 0, 1): 'S', ('du', 0, 1): 'V', ('ho', 1, 1): 'S', ('du', 1, 1): 'V', ('yo', 0, 1): 'S', ('ci', 0, 0): 'V', ('ci', 0, 1): 'S', ('ci', 0, 2): 'V', ('ci', 0, 3): 'S', ('ci', 1, 0): 'V', ('ci', 1, 1): 'V', ('ci', 1, 2): 'S', ('ci', 1, 3): 'V', ('co', 0, 0): 'S', ('co', 1, 0): 'V', ('W', 0, 0): 'V', ('W', 0, 1): 'S', ('W', 0, 2): 'V', ('W', 0, 3): 'S', ('W', 0, 4): 'S', ('W', 0, 5): 'S', ('W', 0, 6): 'S', ('W', 0, 7): 'S', ('W', 1, 0): 'S', ('W', 1, 1): 'V', ('W', 1, 2): 'V', ('W', 1, 3): 'S', ('W', 1, 4): 'S', ('W', 1, 5): 'S', ('W', 1, 6): 'S', ('W', 1, 7): 'S', ('W', 2, 0): 'V', ('W', 2, 1): 'V', ('W', 2, 2): 'S', ('W', 2, 3): 'S', ('W', 2, 4): 'V', ('W', 2, 5): 'S', ('W', 2, 6): 'V', ('W', 2, 7): 'S', ('W', 3, 0): 'V', ('W', 3, 1): 'V', ('W', 3, 2): 'S', ('W', 3, 3): 'V', ('W', 3, 4): 'S', ('W', 3, 5): 'S', ('W', 3, 6): 'S', ('W', 3, 7): 'S'}
-D_STEP = -7
-LOADS = ('Hs', ('H', 0), 'gh', 'd', ('H', 1), ('H', 2), ('C', 0), ('C', 1), ('C', 2), ('H', 3), ('C', 3), ('H', 4), ('u', 0), ('u', 1), ('H', 5), ('u', 2), ('H', 6), ('u', 3), ('H', 7), ('u', 4), ('u', 5), 'W', ('g', 0), ('g', 1), ('u', 6), ('g', 2), ('u', 7), ('g', 3), ('g', 4), ('g', 5), ('g', 6), ('g', 7))
+SCALE_BLOCK = 128
+BLOCKS_PER_PASS = PASS // SCALE_BLOCK
+BANKS = 8
+SCALE_ROWS = 4
+
+GATE_FIRST = 64
+
+STAGES = (
+    ("readout", 1, None),
+    ("turn_h", 0, 5),
+    ("widen", 1, 4),
+    ("quantize_c", 1, 4),
+    ("quantize_h", 0, 6),
+    ("turn_y", None, 10),
+    ("add_skip", 0, 9),
+    ("turn_h", 1, 5),
+    ("sigmoid", None, 12),
+    ("project", 0, 12),
+    ("widen", 3, 4),
+    ("add_skip", 1, 8),
+    ("readout", 0, None),
+    ("group_c", 1, 3),
+    ("apply_gate", 0, 13),
+    ("apply_gate", 1, 13),
+    ("quantize_h", 1, 6),
+    ("empty_h", 0, 5),
+    ("quantize_c", 0, 4),
+    ("skip_term", 1, 7),
+    ("group_c", 0, 3),
+    ("widen", 2, 4),
+    ("empty_h", 1, 5),
+    ("skip_term", 0, 7),
+    ("empty_y", None, 10),
+    ("widen", 0, 3),
+    ("quantize_y", None, 11),
+    ("project", 1, 12),
+)
+STEPS = TILES + max(delay for name, part, delay in STAGES if delay is not None)
+SPREAD_D_STEP = 2
+
+EARLY_TILES = 3
+EARLY_STEPS = 3
+H_STAGES = ("widen", "turn_h", "empty_h", "quantize_h")
+C_STAGES = ("group_c", "quantize_c")
+
+WIDEN_ON_VECTOR = {0: (0, 2, 3), 1: (1, 2, 3), 2: (0, 1), 3: (3,), 4: (2,), 6: (2,)}
+GROUP_ON_VECTOR = ((0, 0), (0, 1), (1, 1), (2, 0), (3, 1))
+
+LATER_LOADS = (
+    "C0 C1 C2 H3 C3 H4 u0 u1 H5 u2 H6 u3 H7 u4 u5 W gate0 gate1 u6 gate2 u7 gate3 gate4 gate5 gate6 gate7"
+).split()
 
 
 def tile_state_space_readout_d4_kernel(tc, H_bytes, H_scale, C, u, d, W_words, W_scales, gate, out):
@@ -46,23 +91,23 @@ def tile_state_space_readout_d4_kernel(tc, H_bytes, H_scale, C, u, d, W_words, W
         psum = ctx.enter_context(tc.psum_pool(name="psum", bufs=1))
         ctx.enter_context(tc.manual_schedule())
 
-        free_banks = list(range(8))
-        held = {}
+        free_banks = list(range(BANKS))
+        bank_of = {}
 
-        def bank(key, shape, dtype=F32):
-            held[key] = free_banks.pop(0)
-            return psum.tile(shape, dtype, name=f"bank{held[key]}")
+        def take_bank(user, shape, dtype=F32):
+            bank_of[user] = free_banks.pop(0)
+            return psum.tile(shape, dtype, name=f"bank{bank_of[user]}")
 
-        def release(key):
-            free_banks.append(held[key])
+        def release_bank(user):
+            free_banks.append(bank_of[user])
 
         ident = keep.tile([P, P], F32, name="ident")
         ones = keep.tile([P, P], BF16, name="ones")
         d_row = keep.tile([P, N], BF16, name="d_row")
         d_all = keep.tile([P, N], BF16, name="d_all")
-        h_scale = keep.tile([P, TILES, BLOCKS], F32, name="h_scale")
+        h_scale = keep.tile([P, TILES, K // SCALE_BLOCK], F32, name="h_scale")
         h_bytes = keep.tile([P, TILES, K], U8, name="h_bytes")
-        c_raw = keep.tile([P, H_PASSES, 4, N], BF16, name="c_raw")
+        c_raw = keep.tile([P, H_PASSES, PACK, N], BF16, name="c_raw")
         u_sb = keep.tile([P, TILES, N], BF16, name="u_sb")
         gate_sb = keep.tile([P, TILES, R], BF16, name="gate_sb")
         w_words = keep.tile([P, Y_PASSES, 2 * R], U8, name="w_words", align_bytes=256)
@@ -77,140 +122,150 @@ def tile_state_space_readout_d4_kernel(tc, H_bytes, H_scale, C, u, d, W_words, W
         nc.vector.memset(ones[:], 1.0)
         nc.gpsimd.memset(w_scales[:].rearrange("p g n -> p (g n)").bitcast(I32), 0)
 
-        def load_rows(dst, src, i0, i1):
-            nc.sync.dma_start(out=dst[:, i0:i1, :], in_=src[:, i0:i1, :])
+        def load_tile(dst, src, i):
+            nc.sync.dma_start(out=dst[:, i : i + 1, :], in_=src[:, i : i + 1, :])
 
-        for item in LOADS:
-            if item == "Hs":
-                nc.sync.dma_start(out=h_scale[:], in_=H_scale.rearrange("(p i) j -> p i j", i=TILES))
-            elif item == "gh":
-                nc.sync.dma_start(out=gate_sb[:, 0, :GATE_HEAD], in_=gate_rows[:, 0, :GATE_HEAD])
-            elif item == "d":
-                nc.scalar.dma_start(out=d_row[0:1, :], in_=d.rearrange("(o n) -> o n", o=1))
-            elif item == "W":
-                for q in range(4):
-                    nc.sync.dma_start(
-                        out=w_scales[32 * q : 32 * q + 4, :, :].bitcast(I32),
-                        in_=W_scales[:, 4 * q : 4 * q + 4, :].rearrange("g r n -> r g n").bitcast(I32),
-                    )
-                nc.sync.dma_start(out=w_words[:].bitcast(I32), in_=W_words.rearrange("g p b -> p g b").bitcast(I32))
-            elif item[0] == "C":
-                g = item[1]
-                nc.sync.dma_start(out=c_raw[:, g, :, :], in_=C[g * PASS : (g + 1) * PASS, :].rearrange("(p j) n -> p j n", j=4))
-            elif item == ("g", 0):
-                nc.sync.dma_start(out=gate_sb[:, 0, GATE_HEAD:], in_=gate_rows[:, 0, GATE_HEAD:])
+        def load_c(g):
+            rows = C[g * PASS : (g + 1) * PASS, :]
+            nc.sync.dma_start(out=c_raw[:, g, :, :], in_=rows.rearrange("(p t) n -> p t n", t=PACK))
+
+        def load_w():
+            for q in range(P // 32):
+                nc.sync.dma_start(
+                    out=w_scales[32 * q : 32 * q + SCALE_ROWS, :, :].bitcast(I32),
+                    in_=W_scales[:, SCALE_ROWS * q : SCALE_ROWS * (q + 1), :].rearrange("g r n -> r g n").bitcast(I32),
+                )
+            nc.sync.dma_start(out=w_words[:].bitcast(I32), in_=W_words.rearrange("g p b -> p g b").bitcast(I32))
+
+        nc.sync.dma_start(out=h_scale[:], in_=H_scale.rearrange("(p i) j -> p i j", i=TILES))
+        load_tile(h_bytes, h_rows, 0)
+        nc.sync.dma_start(out=gate_sb[:, 0, :GATE_FIRST], in_=gate_rows[:, 0, :GATE_FIRST])
+        nc.sync.dma_start(out=d_row[0:1, :], in_=d.rearrange("(o n) -> o n", o=1))
+        for i in range(1, EARLY_TILES):
+            load_tile(h_bytes, h_rows, i)
+        for item in LATER_LOADS:
+            if item == "W":
+                load_w()
+            elif item == "gate0":
+                nc.sync.dma_start(out=gate_sb[:, 0, GATE_FIRST:], in_=gate_rows[:, 0, GATE_FIRST:])
+            elif item.startswith("C"):
+                load_c(int(item[-1]))
             else:
-                dst, src = {"H": (h_bytes, h_rows), "u": (u_sb, u_rows), "g": (gate_sb, gate_rows)}[item[0]]
-                load_rows(dst, src, item[1], item[1] + 1)
+                dst, src = {"H": (h_bytes, h_rows), "u": (u_sb, u_rows), "gate": (gate_sb, gate_rows)}[item[:-1]]
+                load_tile(dst, src, int(item[-1]))
 
-        sig = {}
         h_wide, h_banks, h_turned, c_grouped = {}, {}, {}, {}
-        y_banks, skip, y_sb, y_bank, y_turned, y_codes, y_scales, o_banks = {}, {}, {}, {}, {}, {}, {}, {}
+        y_banks, skip, y_sb, y_pair_bank, y_turned, y_codes, y_scales = {}, {}, {}, {}, {}, {}, {}
+        sig, o_banks = {}, {}
+        quantised = set()
+        passes_done = {}
 
-        def widen(i, blocks, on_vector):
+        def half_cols(h):
+            return slice(h * HALF, (h + 1) * HALF)
+
+        def widen(i, g):
             if i not in h_wide:
                 h_wide[i] = work.tile([P, K], BF16, name="h_wide", bufs=4)
-            for j in blocks:
-                cols = slice(j * BLOCK, (j + 1) * BLOCK)
+            for j in range(BLOCKS_PER_PASS * g, BLOCKS_PER_PASS * (g + 1)):
+                cols = slice(j * SCALE_BLOCK, (j + 1) * SCALE_BLOCK)
                 src = h_bytes[:, i, cols].bitcast(FP8)
                 scale = h_scale[:, i, j : j + 1]
-                if on_vector:
+                if g in WIDEN_ON_VECTOR.get(i, ()):
                     nc.vector.tensor_scalar(out=h_wide[i][:, cols], in0=src, scalar1=scale, scalar2=None, op0=ALU.mult)
                 else:
                     nc.scalar.activation(out=h_wide[i][:, cols], in_=src, func=ACT.Copy, scale=scale)
 
         def turn_h(i, b):
-            words = h_wide[i][:].bitcast(F32)
-            h_banks[i, b] = bank(("h", i, b), [P, 2, 2, P])
+            pairs = h_wide[i][:].bitcast(F32)
+            h_banks[i, b] = take_bank(("h", i, b), [P, 2, 2, P])
             for gg in range(2):
                 g = 2 * b + gg
                 for w in range(2):
-                    nc.tensor.transpose(h_banks[i, b][:, gg, w, :], words[:, 256 * g + w : 256 * (g + 1) : 2], ident[:])
+                    nc.tensor.transpose(h_banks[i, b][:, gg, w, :], pairs[:, PAIRS * g + w : PAIRS * (g + 1) : 2], ident[:])
 
-        def empty_h(i, b, e):
-            h_turned[i, b] = work.tile([P, 2 * P * 4], BF16, name="h_turned", bufs=4, align_bytes=256)
-            dst = h_turned[i, b][:].bitcast(F32).rearrange("p (g t w) -> p g t w", g=2, w=2)
-            src = h_banks[i, b][:].rearrange("p g w t -> p g t w")
-            if e == "V":
-                nc.vector.tensor_copy(out=dst, in_=src)
-            else:
-                nc.scalar.copy(out=dst, in_=src)
-            release(("h", i, b))
+        def empty_pairs(dst, src_bank):
+            nc.scalar.copy(
+                out=dst[:].bitcast(F32).rearrange("p (g tok w) -> p g tok w", g=2, w=2),
+                in_=src_bank[:].rearrange("p g w tok -> p g tok w"),
+            )
+
+        def empty_h(i, b):
+            h_turned[i, b] = work.tile([P, 2 * P * PACK], BF16, name="h_turned", bufs=4, align_bytes=256)
+            empty_pairs(h_turned[i, b], h_banks[i, b])
+            release_bank(("h", i, b))
 
         def quantize_h(i, b):
             cols = slice(2 * b * P, 2 * (b + 1) * P)
             nc.vector.quantize_mx(out=h_codes[:, i, cols].bitcast(FP8X4), scales=h_scales[:, i, cols], in_=h_turned[i, b][:])
+            quantised.add(("h", i, b))
 
-        def group_c(g, h, e):
-            c_grouped[g, h] = work.tile([P, HALF * 4], BF16, name="c_grouped", bufs=4, align_bytes=256)
-            dst = c_grouped[g, h][:].rearrange("p (w m e j) -> p m j w e", w=2, e=2, j=4)
-            src = c_raw[:, g, :, h * HALF : (h + 1) * HALF].rearrange("p j (m w e) -> p m j w e", w=2, e=2)
-            if e == "V":
+        def group_c(g, h):
+            c_grouped[g, h] = work.tile([P, HALF * PACK], BF16, name="c_grouped", bufs=4, align_bytes=256)
+            dst = c_grouped[g, h][:].rearrange("p (w m e t) -> p m t w e", w=2, e=2, t=PACK)
+            src = c_raw[:, g, :, half_cols(h)].rearrange("p t (m w e) -> p m t w e", w=2, e=2)
+            if (g, h) in GROUP_ON_VECTOR:
                 nc.vector.tensor_copy(out=dst, in_=src)
             else:
                 nc.scalar.copy(out=dst, in_=src)
 
         def quantize_c(g, h):
-            cols = slice(h * HALF, (h + 1) * HALF)
+            cols = half_cols(h)
             nc.vector.quantize_mx(out=c_codes[:, g, cols].bitcast(FP8X4), scales=c_scales[:, g, cols], in_=c_grouped[g, h][:])
+            quantised.add(("c", g, h))
 
-        def readout(i, h, g):
-            if g == 0:
-                y_banks[i, h] = bank(("y", i, h), [P, HALF])
-            tok = slice(g * P, (g + 1) * P)
-            cols = slice(h * HALF, (h + 1) * HALF)
-            nc.tensor.matmul_mx(
-                out=y_banks[i, h][:],
-                lhsT=h_codes[:, i, tok].bitcast(FP8X4),
-                lhsT_scale=h_scales[:, i, tok],
-                rhs=c_codes[:, g, cols].bitcast(FP8X4),
-                rhs_scale=c_scales[:, g, cols],
-                start=(g == 0),
-                stop=(g == H_PASSES - 1),
-            )
+        def readout(h):
+            for i in range(TILES):
+                for g in range(passes_done.get((i, h), 0), H_PASSES):
+                    if ("h", i, g // 2) not in quantised or ("c", g, h) not in quantised:
+                        break
+                    if g == 0:
+                        y_banks[i, h] = take_bank(("y", i, h), [P, HALF])
+                    tokens = slice(g * P, (g + 1) * P)
+                    nc.tensor.matmul_mx(
+                        out=y_banks[i, h][:],
+                        lhsT=h_codes[:, i, tokens].bitcast(FP8X4),
+                        lhsT_scale=h_scales[:, i, tokens],
+                        rhs=c_codes[:, g, half_cols(h)].bitcast(FP8X4),
+                        rhs_scale=c_scales[:, g, half_cols(h)],
+                        start=(g == 0),
+                        stop=(g == H_PASSES - 1),
+                    )
+                    passes_done[i, h] = g + 1
 
         def spread_d():
-            acc = bank("d", [P, N], BF16)
-            for h in range(HALVES):
-                cols = slice(h * HALF, (h + 1) * HALF)
-                nc.tensor.matmul(acc[:, cols], lhsT=ones[:], rhs=d_row[:, cols], start=True, stop=True)
+            acc = take_bank("d", [P, N], BF16)
+            for h in range(N // HALF):
+                nc.tensor.matmul(acc[:, half_cols(h)], lhsT=ones[:], rhs=d_row[:, half_cols(h)], start=True, stop=True)
             nc.scalar.copy(out=d_all[:], in_=acc[:])
-            release("d")
+            release_bank("d")
 
-        def skip_term(i, h, e):
-            cols = slice(h * HALF, (h + 1) * HALF)
+        def skip_term(i, h):
             skip[i, h] = work.tile([P, HALF], F32, name="skip", bufs=4)
-            eng = nc.gpsimd if e == "G" else nc.vector
-            eng.tensor_tensor(out=skip[i, h][:], in0=u_sb[:, i, cols], in1=d_all[:, cols], op=ALU.mult)
+            nc.vector.tensor_tensor(out=skip[i, h][:], in0=u_sb[:, i, half_cols(h)], in1=d_all[:, half_cols(h)], op=ALU.mult)
 
         def add_skip(i, h):
             if i not in y_sb:
                 y_sb[i] = work.tile([P, N], BF16, name="y_sb", bufs=4)
             nc.vector.tensor_tensor(
-                out=y_sb[i][:, h * HALF : (h + 1) * HALF].rearrange("p (w m e) -> p w m e", w=2, e=2),
+                out=y_sb[i][:, half_cols(h)].rearrange("p (w m e) -> p w m e", w=2, e=2),
                 in0=y_banks[i, h][:].rearrange("p (w m e) -> p w m e", w=2, e=2),
                 in1=skip[i, h][:].rearrange("p (m w e) -> p w m e", w=2, e=2),
                 op=ALU.add,
             )
-            release(("y", i, h))
+            release_bank(("y", i, h))
 
         def turn_y(i):
-            words = y_sb[i][:].bitcast(F32)
-            y_bank[i] = bank(("t", i), [P, 2, 2, P])
+            pairs = y_sb[i][:].bitcast(F32)
+            y_pair_bank[i] = take_bank(("y pairs", i), [P, 2, 2, P])
             for g in range(Y_PASSES):
                 for w in range(2):
-                    c0 = 256 * g + P * w
-                    nc.tensor.transpose(y_bank[i][:, g, w, :], words[:, c0 : c0 + P], ident[:])
+                    first = PAIRS * g + P * w
+                    nc.tensor.transpose(y_pair_bank[i][:, g, w, :], pairs[:, first : first + P], ident[:])
 
-        def empty_y(i, e):
-            y_turned[i] = work.tile([P, 2 * P * 4], BF16, name="y_turned", align_bytes=256)
-            dst = y_turned[i][:].bitcast(F32).rearrange("p (g t w) -> p g t w", g=2, w=2)
-            src = y_bank[i][:].rearrange("p g w t -> p g t w")
-            if e == "V":
-                nc.vector.tensor_copy(out=dst, in_=src)
-            else:
-                nc.scalar.copy(out=dst, in_=src)
-            release(("t", i))
+        def empty_y(i):
+            y_turned[i] = work.tile([P, 2 * P * PACK], BF16, name="y_turned", align_bytes=256)
+            empty_pairs(y_turned[i], y_pair_bank[i])
+            release_bank(("y pairs", i))
 
         def quantize_y(i):
             y_codes[i] = work.tile([P, Y_PASSES * P], U32, name="y_codes", bufs=3, align_bytes=256)
@@ -218,87 +273,69 @@ def tile_state_space_readout_d4_kernel(tc, H_bytes, H_scale, C, u, d, W_words, W
             nc.vector.quantize_mx(out=y_codes[i][:].bitcast(FP8X4), scales=y_scales[i][:], in_=y_turned[i][:])
 
         def project(i, h):
-            o_banks[i, h] = bank(("o", i, h), [P, HALF])
+            o_banks[i, h] = take_bank(("o", i, h), [P, HALF])
             for g in range(Y_PASSES):
-                tok = slice(g * P, (g + 1) * P)
+                tokens = slice(g * P, (g + 1) * P)
                 nc.tensor.matmul_mx(
                     out=o_banks[i, h][:],
-                    lhsT=y_codes[i][:, tok].bitcast(FP8X4),
-                    lhsT_scale=y_scales[i][:, tok],
+                    lhsT=y_codes[i][:, tokens].bitcast(FP8X4),
+                    lhsT_scale=y_scales[i][:, tokens],
                     rhs=w_words[:, g, 2 * h * HALF : 2 * (h + 1) * HALF].bitcast(FP4X4),
-                    rhs_scale=w_scales[:, g, h * HALF : (h + 1) * HALF],
+                    rhs_scale=w_scales[:, g, half_cols(h)],
                     start=(g == 0),
                     stop=(g == Y_PASSES - 1),
                 )
 
-        def squash(i, c0, c1):
+        def sigmoid_cols(i, cols):
             if i not in sig:
                 sig[i] = work.tile([P, R], F32, name="sig", bufs=4)
-            nc.scalar.activation(out=sig[i][:, c0:c1], in_=gate_sb[:, i, c0:c1], func=ACT.Sigmoid)
+            nc.scalar.activation(out=sig[i][:, cols], in_=gate_sb[:, i, cols], func=ACT.Sigmoid)
+
+        def sigmoid(i):
+            sigmoid_cols(i, slice(GATE_FIRST if i == 0 else 0, R))
 
         def apply_gate(i, h):
             o_sb = work.tile([P, HALF], F32, name="o_sb", bufs=8)
-            cols = slice(h * HALF, (h + 1) * HALF)
-            nc.vector.tensor_tensor(out=o_sb[:], in0=o_banks[i, h][:], in1=sig[i][:, cols], op=ALU.mult)
-            release(("o", i, h))
-            nc.sync.dma_start(out=out_rows[:, i, cols], in_=o_sb[:])
+            nc.vector.tensor_tensor(out=o_sb[:], in0=o_banks[i, h][:], in1=sig[i][:, half_cols(h)], op=ALU.mult)
+            release_bank(("o", i, h))
+            nc.sync.dma_start(out=out_rows[:, i, half_cols(h)], in_=o_sb[:])
 
-        squash(0, 0, GATE_HEAD)
-        done = set()
-        for s in range(-9, 12):
-            if s == D_STEP:
+        stage = {
+            "widen": widen,
+            "turn_h": turn_h,
+            "empty_h": empty_h,
+            "quantize_h": quantize_h,
+            "group_c": group_c,
+            "quantize_c": quantize_c,
+            "skip_term": skip_term,
+            "add_skip": add_skip,
+            "turn_y": turn_y,
+            "empty_y": empty_y,
+            "quantize_y": quantize_y,
+            "sigmoid": sigmoid,
+            "project": project,
+            "apply_gate": apply_gate,
+        }
+
+        def index_at(name, step, delay):
+            index = step - delay
+            if name in H_STAGES and index < EARLY_TILES:
+                index += EARLY_STEPS
+                return index if 0 <= index < EARLY_TILES else None
+            return index if 0 <= index < (H_PASSES if name in C_STAGES else TILES) else None
+
+        sigmoid_cols(0, slice(0, GATE_FIRST))
+        for step in range(STEPS):
+            if step == SPREAD_D_STEP:
                 spread_d()
-            for k, a, off in TEMPLATE:
-                i = s + off
-                if k in ("ci", "cq"):
-                    if 0 <= i < H_PASSES:
-                        if k == "ci":
-                            group_c(i, a, ENG["ci", a, i])
-                        else:
-                            quantize_c(i, a)
-                        done.add((k, i, a))
+            for name, part, delay in STAGES:
+                if name == "readout":
+                    readout(part)
                     continue
-                if k == "m1":
-                    for j in range(0, min(max(i, ENG["k"] - 1), TILES - 1) + 1):
-                        for g in range(H_PASSES):
-                            if ("m1", j, a, g) in done:
-                                continue
-                            if ("hq", j, g // 2) in done and ("cq", g, a) in done:
-                                readout(j, a, g)
-                                done.add(("m1", j, a, g))
-                            else:
-                                break
+                index = index_at(name, step, delay)
+                if index is None:
                     continue
-                if k in ("w", "th", "ho", "hq"):
-                    if 0 <= i + ENG["gap"] < ENG["k"]:
-                        i += ENG["gap"]
-                    elif i < ENG["k"]:
-                        continue
-                if not 0 <= i < TILES:
-                    continue
-                ph = 0 if i < ENG["phd" if k == "du" else "ph"] else 1
-                if k == "w":
-                    widen(i, range(4 * a, 4 * a + 4), ENG["W", a, i] == "V")
-                elif k == "th":
-                    turn_h(i, a)
-                elif k == "ho":
-                    empty_h(i, a, ENG["ho", a, ph])
-                elif k == "hq":
-                    quantize_h(i, a)
-                    done.add((k, i, a))
-                elif k == "du":
-                    skip_term(i, a, ENG["du", a, ph])
-                elif k == "ya":
-                    add_skip(i, a)
-                elif k == "ty":
-                    turn_y(i)
-                elif k == "yo":
-                    empty_y(i, ENG["yo", 0, ph])
-                elif k == "yq":
-                    quantize_y(i)
-                elif k == "sg":
-                    squash(i, GATE_HEAD if i == 0 else 0, R)
-                elif k == "m2":
-                    project(i, a)
+                if part is None:
+                    stage[name](index)
                 else:
-                    apply_gate(i, a)
+                    stage[name](index, part)

@@ -8,334 +8,490 @@ FLOPS = 2 * T * K * N + 2 * T * N * R
 
 F32 = mybir.dt.float32
 BF16 = mybir.dt.bfloat16
-U8 = mybir.dt.uint8
 U32 = mybir.dt.uint32
 I32 = mybir.dt.int32
+U8 = mybir.dt.uint8
 FP8 = mybir.dt.float8_e4m3fn
 FP8X4 = mybir.dt.float8_e4m3fn_x4
 FP4X4 = mybir.dt.float4_e2m1fn_x4
-ACT = mybir.ActivationFunctionType
 ALU = mybir.AluOpType
+ACT = mybir.ActivationFunctionType
 
 P = 128
-TILES = T // P
 PACK = 4
-PASS = P * PACK
-PAIRS = PASS // 2
-H_PASSES = K // PASS
-Y_PASSES = N // PASS
-HALF = 512
-SCALE_BLOCK = 128
-BLOCKS_PER_PASS = PASS // SCALE_BLOCK
-BANKS = 8
-SCALE_ROWS = 4
+KP = P * PACK
+TILES = T // P
+PAIR = 2
+GT = PAIR * P
+GROUPS = TILES // PAIR
+PASSES = K // KP
+HALVES = N // KP
+BLK = 128
 
-GATE_FIRST = 64
-
-STAGES = (
-    ("readout", 1, None),
-    ("turn_h", 0, 5),
-    ("widen", 1, 4),
-    ("quantize_c", 1, 4),
-    ("quantize_h", 0, 6),
-    ("turn_y", None, 10),
-    ("add_skip", 0, 9),
-    ("turn_h", 1, 5),
-    ("sigmoid", None, 12),
-    ("project", 0, 12),
-    ("widen", 3, 4),
-    ("add_skip", 1, 8),
-    ("readout", 0, None),
-    ("group_c", 1, 3),
-    ("apply_gate", 0, 13),
-    ("apply_gate", 1, 13),
-    ("quantize_h", 1, 6),
-    ("empty_h", 0, 5),
-    ("quantize_c", 0, 4),
-    ("skip_term", 1, 7),
-    ("group_c", 0, 3),
-    ("widen", 2, 4),
-    ("empty_h", 1, 5),
-    ("skip_term", 0, 7),
-    ("empty_y", None, 10),
-    ("widen", 0, 3),
-    ("quantize_y", None, 11),
-    ("project", 1, 12),
-)
-STEPS = TILES + max(delay for name, part, delay in STAGES if delay is not None)
-SPREAD_D_STEP = 2
-
-EARLY_TILES = 3
-EARLY_STEPS = 3
-H_STAGES = ("widen", "turn_h", "empty_h", "quantize_h")
-C_STAGES = ("group_c", "quantize_c")
-
-WIDEN_ON_VECTOR = {0: (0, 2, 3), 1: (1, 2, 3), 2: (0, 1), 3: (3,), 4: (2,), 6: (2,)}
-GROUP_ON_VECTOR = ((0, 0), (0, 1), (1, 1), (2, 0), (3, 1))
-
-LATER_LOADS = (
-    "C0 C1 C2 H3 C3 H4 u0 u1 H5 u2 H6 u3 H7 u4 u5 W gate0 gate1 u6 gate2 u7 gate3 gate4 gate5 gate6 gate7"
-).split()
+EVAC_V = (("u", 0, 0), ("u", 0, 1), ("u", 1, 0),)
+YIL_G = ()
+LAG = 3
+TB, YB, OB = 2, 3, 3
+WIDEN_S = (1,)
+CIL_V = ((1, 0), (1, 2),)
+YIL_S = ((0, 0), (1, 0), (2, 0), (1, 1), (3, 0), (2, 1),)
 
 
 def tile_state_space_readout_d4_kernel(tc, H_bytes, H_scale, C, u, d, W_words, W_scales, gate, out):
     nc = tc.nc
-    h_rows = H_bytes.rearrange("(p i) k -> p i k", i=TILES)
-    u_rows = u.rearrange("(p i) n -> p i n", i=TILES)
-    gate_rows = gate.rearrange("(p i) n -> p i n", i=TILES)
-    out_rows = out.rearrange("(p i) n -> p i n", i=TILES)
-
     with ExitStack() as ctx:
         keep = ctx.enter_context(tc.tile_pool(name="keep", bufs=1))
         work = ctx.enter_context(tc.tile_pool(name="work", bufs=2))
         psum = ctx.enter_context(tc.psum_pool(name="psum", bufs=1))
         ctx.enter_context(tc.manual_schedule())
 
-        free_banks = list(range(BANKS))
-        bank_of = {}
-
-        def take_bank(user, shape, dtype=F32):
-            bank_of[user] = free_banks.pop(0)
-            return psum.tile(shape, dtype, name=f"bank{bank_of[user]}")
-
-        def release_bank(user):
-            free_banks.append(bank_of[user])
+        h_rows = H_bytes.rearrange("(p j) k -> p j k", j=TILES)
+        u_rows = u.rearrange("(p j) n -> p j n", j=TILES)
+        g_rows = gate.rearrange("(p j) r -> p j r", j=TILES)
+        o_rows = out.rearrange("(p j) r -> p j r", j=TILES)
 
         ident = keep.tile([P, P], F32, name="ident")
-        ones = keep.tile([P, P], BF16, name="ones")
-        d_row = keep.tile([P, N], BF16, name="d_row")
-        d_all = keep.tile([P, N], BF16, name="d_all")
-        h_scale = keep.tile([P, TILES, K // SCALE_BLOCK], F32, name="h_scale")
-        h_bytes = keep.tile([P, TILES, K], U8, name="h_bytes")
-        c_raw = keep.tile([P, H_PASSES, PACK, N], BF16, name="c_raw")
-        u_sb = keep.tile([P, TILES, N], BF16, name="u_sb")
-        gate_sb = keep.tile([P, TILES, R], BF16, name="gate_sb")
-        w_words = keep.tile([P, Y_PASSES, 2 * R], U8, name="w_words", align_bytes=256)
-        w_scales = keep.tile([P, Y_PASSES, R], U8, name="w_scales", align_bytes=256)
-        c_codes = keep.tile([P, H_PASSES, N], U32, name="c_codes", align_bytes=256)
-        c_scales = keep.tile([P, H_PASSES, N], U8, name="c_scales", align_bytes=256)
-        h_codes = keep.tile([P, TILES, H_PASSES * P], U32, name="h_codes", align_bytes=256)
-        h_scales = keep.tile([P, TILES, H_PASSES * P], U8, name="h_scales", align_bytes=256)
-
+        w_scale = keep.tile([P, HALVES, R], U8, name="w_scale", align_bytes=64)
+        warm = keep.tile([P, 2], F32, name="warm")
         make_identity(nc, ident[:])
-        nc.vector.memset(d_row[:].bitcast(I32), 0)
-        nc.vector.memset(ones[:], 1.0)
-        nc.gpsimd.memset(w_scales[:].rearrange("p g n -> p (g n)").bitcast(I32), 0)
+        nc.scalar.activation(out=warm[:], in_=ident[:, 0:2], func=ACT.Sigmoid)
+        ident16 = keep.tile([P, P], BF16, name="ident16")
+        make_identity(nc, ident16[:])
+        nc.gpsimd.memset(w_scale[:].rearrange("p h r -> p (h r)").bitcast(I32), 0)
 
-        def load_tile(dst, src, i):
-            nc.sync.dma_start(out=dst[:, i : i + 1, :], in_=src[:, i : i + 1, :])
+        h_scale = keep.tile([P, TILES * K // BLK], F32, name="h_scale")
+        d_col = keep.tile([P, HALVES, PACK], BF16, name="d_col")
+        w_words = keep.tile([P, HALVES, 2 * R], U8, name="w_words", align_bytes=64)
+        h_raw, c_raw, u_raw, g_raw = {}, {}, {}, {}
+        h_wide, h_in, h_code, h_sc, c_in, c_code, c_sc = {}, {}, {}, {}, {}, {}, {}
+        t_bank = {}
+        u_t, y_bank, y_pl, y_in, y_code, y_sc, sig, o_bank, res = {}, {}, {}, {}, {}, {}, {}, {}, {}
 
-        def load_c(g):
-            rows = C[g * PASS : (g + 1) * PASS, :]
-            nc.sync.dma_start(out=c_raw[:, g, :, :], in_=rows.rearrange("(p t) n -> p t n", t=PACK))
+        def load_h(j):
+            h_raw[j] = keep.tile([P, K], U8, name="h_raw%d" % j)
+            nc.sync.dma_start(out=h_raw[j][:], in_=h_rows[:, j, :])
+
+        def load_c(h, g):
+            c_raw[h, g] = keep.tile([P, PACK, KP], BF16, name="c_raw%d_%d" % (h, g))
+            rows = C[g * KP:(g + 1) * KP, h * KP:(h + 1) * KP]
+            nc.sync.dma_start(out=c_raw[h, g][:], in_=rows.rearrange("(p j) n -> p j n", j=PACK))
+
+        def load_u(q):
+            u_raw[q] = work.tile([P, PAIR * N], BF16, name="u_raw%d" % q, tag="rows", bufs=8)
+            nc.sync.dma_start(out=u_raw[q][:], in_=u_rows[:, PAIR * q:PAIR * (q + 1), :].rearrange("p j n -> p (j n)"))
+
+        def load_g(q):
+            g_raw[q] = work.tile([P, PAIR * R], BF16, name="g_raw%d" % q, tag="rows", bufs=8)
+            nc.sync.dma_start(out=g_raw[q][:], in_=g_rows[:, PAIR * q:PAIR * (q + 1), :].rearrange("p j n -> p (j n)"))
 
         def load_w():
-            for q in range(P // 32):
+            nc.sync.dma_start(out=w_words[:], in_=W_words.rearrange("h p b -> p h b"))
+            for quad in range(4):
                 nc.sync.dma_start(
-                    out=w_scales[32 * q : 32 * q + SCALE_ROWS, :, :].bitcast(I32),
-                    in_=W_scales[:, SCALE_ROWS * q : SCALE_ROWS * (q + 1), :].rearrange("g r n -> r g n").bitcast(I32),
+                    out=w_scale[32 * quad:32 * quad + 4, :, :].bitcast(I32),
+                    in_=W_scales[:, 4 * quad:4 * quad + 4, :].rearrange("h q r -> q h r").bitcast(I32),
                 )
-            nc.sync.dma_start(out=w_words[:].bitcast(I32), in_=W_words.rearrange("g p b -> p g b").bitcast(I32))
 
-        nc.sync.dma_start(out=h_scale[:], in_=H_scale.rearrange("(p i) j -> p i j", i=TILES))
-        load_tile(h_bytes, h_rows, 0)
-        nc.sync.dma_start(out=gate_sb[:, 0, :GATE_FIRST], in_=gate_rows[:, 0, :GATE_FIRST])
-        nc.sync.dma_start(out=d_row[0:1, :], in_=d.rearrange("(o n) -> o n", o=1))
-        for i in range(1, EARLY_TILES):
-            load_tile(h_bytes, h_rows, i)
-        for item in LATER_LOADS:
-            if item == "W":
-                load_w()
-            elif item == "gate0":
-                nc.sync.dma_start(out=gate_sb[:, 0, GATE_FIRST:], in_=gate_rows[:, 0, GATE_FIRST:])
-            elif item.startswith("C"):
-                load_c(int(item[-1]))
-            else:
-                dst, src = {"H": (h_bytes, h_rows), "u": (u_sb, u_rows), "gate": (gate_sb, gate_rows)}[item[:-1]]
-                load_tile(dst, src, int(item[-1]))
+        def widen(j, gs=range(PASSES)):
+            if j not in h_wide:
+                h_wide[j] = work.tile([P, K], BF16, name="h_wide%d" % j, tag="h_wide", bufs=4)
+            for g in gs:
+                for b in range(KP // BLK):
+                    blk = g * (KP // BLK) + b
+                    src = h_raw[j][:, blk * BLK:(blk + 1) * BLK].bitcast(FP8)
+                    col = j * (K // BLK) + blk
+                    if j in WIDEN_S:
+                        nc.scalar.activation(out=h_wide[j][:, blk * BLK:(blk + 1) * BLK], in_=src, func=ACT.Copy,
+                                             scale=h_scale[:, col:col + 1])
+                    else:
+                        dst = h_wide[j][:, g * KP:(g + 1) * KP].rearrange("p (w m e) -> p m w e", w=2, e=2)
+                        nc.vector.tensor_scalar(out=dst[:, 32 * b:32 * (b + 1), :, :], in0=src.rearrange("p (m w e) -> p m w e", w=2, e=2),
+                                                scalar1=h_scale[:, col:col + 1], scalar2=None, op0=ALU.mult)
 
-        h_wide, h_banks, h_turned, c_grouped = {}, {}, {}, {}
-        y_banks, skip, y_sb, y_pair_bank, y_turned, y_codes, y_scales = {}, {}, {}, {}, {}, {}, {}
-        sig, o_banks = {}, {}
-        quantised = set()
-        passes_done = {}
-
-        def half_cols(h):
-            return slice(h * HALF, (h + 1) * HALF)
-
-        def widen(i, g):
-            if i not in h_wide:
-                h_wide[i] = work.tile([P, K], BF16, name="h_wide", bufs=4)
-            for j in range(BLOCKS_PER_PASS * g, BLOCKS_PER_PASS * (g + 1)):
-                cols = slice(j * SCALE_BLOCK, (j + 1) * SCALE_BLOCK)
-                src = h_bytes[:, i, cols].bitcast(FP8)
-                scale = h_scale[:, i, j : j + 1]
-                if g in WIDEN_ON_VECTOR.get(i, ()):
-                    nc.vector.tensor_scalar(out=h_wide[i][:, cols], in0=src, scalar1=scale, scalar2=None, op0=ALU.mult)
-                else:
-                    nc.scalar.activation(out=h_wide[i][:, cols], in_=src, func=ACT.Copy, scale=scale)
-
-        def turn_h(i, b):
-            pairs = h_wide[i][:].bitcast(F32)
-            h_banks[i, b] = take_bank(("h", i, b), [P, 2, 2, P])
-            for gg in range(2):
-                g = 2 * b + gg
+        def turn_h(q, g):
+            bank = psum.tile([P, 2, GT], F32, name="tb_h%d_%d" % (q, g), tag="bank", bufs=8)
+            for i in range(PAIR):
+                j = PAIR * q + i
+                words = h_wide[j][:].bitcast(F32)
                 for w in range(2):
-                    nc.tensor.transpose(h_banks[i, b][:, gg, w, :], pairs[:, PAIRS * g + w : PAIRS * (g + 1) : 2], ident[:])
+                    if j in WIDEN_S:
+                        src = words[:, 256 * g + w:256 * (g + 1):2]
+                    else:
+                        src = words[:, 256 * g + 128 * w:256 * g + 128 * (w + 1)]
+                    nc.tensor.transpose(bank[:, w, i * P:(i + 1) * P], src, ident[:])
+            t_bank["h", q, g] = bank
 
-        def empty_pairs(dst, src_bank):
-            nc.scalar.copy(
-                out=dst[:].bitcast(F32).rearrange("p (g tok w) -> p g tok w", g=2, w=2),
-                in_=src_bank[:].rearrange("p g w tok -> p g tok w"),
-            )
-
-        def empty_h(i, b):
-            h_turned[i, b] = work.tile([P, 2 * P * PACK], BF16, name="h_turned", bufs=4, align_bytes=256)
-            empty_pairs(h_turned[i, b], h_banks[i, b])
-            release_bank(("h", i, b))
-
-        def quantize_h(i, b):
-            cols = slice(2 * b * P, 2 * (b + 1) * P)
-            nc.vector.quantize_mx(out=h_codes[:, i, cols].bitcast(FP8X4), scales=h_scales[:, i, cols], in_=h_turned[i, b][:])
-            quantised.add(("h", i, b))
-
-        def group_c(g, h):
-            c_grouped[g, h] = work.tile([P, HALF * PACK], BF16, name="c_grouped", bufs=4, align_bytes=256)
-            dst = c_grouped[g, h][:].rearrange("p (w m e t) -> p m t w e", w=2, e=2, t=PACK)
-            src = c_raw[:, g, :, half_cols(h)].rearrange("p t (m w e) -> p m t w e", w=2, e=2)
-            if (g, h) in GROUP_ON_VECTOR:
+        def evac_h(q, g):
+            bank = t_bank["h", q, g]
+            h_in[q, g] = work.tile([P, GT * PACK], BF16, name="h_in%d_%d" % (q, g), tag="h_in", bufs=6, align_bytes=64)
+            dst = h_in[q, g][:].bitcast(F32).rearrange("p (r w) -> p r w", w=2)
+            src = bank[:].rearrange("p w r -> p r w")
+            if ("h", q, g) in EVAC_V:
                 nc.vector.tensor_copy(out=dst, in_=src)
             else:
                 nc.scalar.copy(out=dst, in_=src)
 
-        def quantize_c(g, h):
-            cols = half_cols(h)
-            nc.vector.quantize_mx(out=c_codes[:, g, cols].bitcast(FP8X4), scales=c_scales[:, g, cols], in_=c_grouped[g, h][:])
-            quantised.add(("c", g, h))
+        def quant_h(q, g):
+            h_code[q, g] = keep.tile([P, GT], U32, name="h_code%d_%d" % (q, g), align_bytes=64)
+            h_sc[q, g] = keep.tile([P, GT], U8, name="h_sc%d_%d" % (q, g), align_bytes=64)
+            nc.vector.quantize_mx(out=h_code[q, g][:].bitcast(FP8X4), scales=h_sc[q, g][:], in_=h_in[q, g][:])
 
-        def readout(h):
-            for i in range(TILES):
-                for g in range(passes_done.get((i, h), 0), H_PASSES):
-                    if ("h", i, g // 2) not in quantised or ("c", g, h) not in quantised:
-                        break
-                    if g == 0:
-                        y_banks[i, h] = take_bank(("y", i, h), [P, HALF])
-                    tokens = slice(g * P, (g + 1) * P)
-                    nc.tensor.matmul_mx(
-                        out=y_banks[i, h][:],
-                        lhsT=h_codes[:, i, tokens].bitcast(FP8X4),
-                        lhsT_scale=h_scales[:, i, tokens],
-                        rhs=c_codes[:, g, half_cols(h)].bitcast(FP8X4),
-                        rhs_scale=c_scales[:, g, half_cols(h)],
-                        start=(g == 0),
-                        stop=(g == H_PASSES - 1),
-                    )
-                    passes_done[i, h] = g + 1
+        def weave_c(h, g):
+            c_in[h, g] = work.tile([P, KP * PACK], BF16, name="c_in%d_%d" % (h, g), tag="c_in", bufs=4, align_bytes=64)
+            dst = c_in[h, g][:].rearrange("p (t m j) -> p m j t", t=PACK, j=PACK)
+            src = c_raw[h, g][:].rearrange("p j (m t) -> p m j t", t=PACK)
+            if (h, g) in CIL_V:
+                nc.vector.tensor_copy(out=dst, in_=src)
+            else:
+                nc.scalar.copy(out=dst, in_=src)
 
-        def spread_d():
-            acc = take_bank("d", [P, N], BF16)
-            for h in range(N // HALF):
-                nc.tensor.matmul(acc[:, half_cols(h)], lhsT=ones[:], rhs=d_row[:, half_cols(h)], start=True, stop=True)
-            nc.scalar.copy(out=d_all[:], in_=acc[:])
-            release_bank("d")
+        def pweave_c(h, g, w):
+            bank = psum.tile([P, 2, KP], BF16, name="cb%d_%d_%d" % (h, g, w), tag="bank", bufs=8)
+            t_bank["c", h, g, w] = bank
+            src = c_raw[h, g][:].rearrange("p j (m t) -> p t m j", t=PACK)
+            for e in range(2):
+                nc.tensor.matmul(out=bank[:, e, :], lhsT=ident16[:], rhs=src[:, 2 * w + e, :, :], start=True, stop=True)
 
-        def skip_term(i, h):
-            skip[i, h] = work.tile([P, HALF], F32, name="skip", bufs=4)
-            nc.vector.tensor_tensor(out=skip[i, h][:], in0=u_sb[:, i, half_cols(h)], in1=d_all[:, half_cols(h)], op=ALU.mult)
+        def evac_c(h, g, w):
+            if w == 0:
+                c_in[h, g] = work.tile([P, KP * PACK], BF16, name="c_in%d_%d" % (h, g), tag="c_in", bufs=4, align_bytes=64)
+            dst = c_in[h, g][:, 2 * KP * w:2 * KP * (w + 1)]
+            src = t_bank["c", h, g, w][:].rearrange("p e n -> p (e n)")
+            if ("c", h, g, w) in EVAC_V:
+                nc.vector.tensor_copy(out=dst, in_=src)
+            else:
+                nc.scalar.copy(out=dst, in_=src)
 
-        def add_skip(i, h):
-            if i not in y_sb:
-                y_sb[i] = work.tile([P, N], BF16, name="y_sb", bufs=4)
-            nc.vector.tensor_tensor(
-                out=y_sb[i][:, half_cols(h)].rearrange("p (w m e) -> p w m e", w=2, e=2),
-                in0=y_banks[i, h][:].rearrange("p (w m e) -> p w m e", w=2, e=2),
-                in1=skip[i, h][:].rearrange("p (m w e) -> p w m e", w=2, e=2),
-                op=ALU.add,
-            )
-            release_bank(("y", i, h))
+        def quant_c(h, g):
+            c_code[h, g] = keep.tile([P, KP], U32, name="c_code%d_%d" % (h, g), align_bytes=64)
+            c_sc[h, g] = keep.tile([P, KP], U8, name="c_sc%d_%d" % (h, g), align_bytes=64)
+            nc.vector.quantize_mx(out=c_code[h, g][:].bitcast(FP8X4), scales=c_sc[h, g][:], in_=c_in[h, g][:])
 
-        def turn_y(i):
-            pairs = y_sb[i][:].bitcast(F32)
-            y_pair_bank[i] = take_bank(("y pairs", i), [P, 2, 2, P])
-            for g in range(Y_PASSES):
+        def turn_u(q, h):
+            bank = psum.tile([P, 2, GT], F32, name="tb_u%d_%d" % (q, h), tag="bank", bufs=8)
+            words = u_raw[q][:].bitcast(F32)
+            for i in range(PAIR):
                 for w in range(2):
-                    first = PAIRS * g + P * w
-                    nc.tensor.transpose(y_pair_bank[i][:, g, w, :], pairs[:, first : first + P], ident[:])
+                    base = i * (N // 2) + 256 * h
+                    nc.tensor.transpose(bank[:, w, i * P:(i + 1) * P], words[:, base + w:base + 256:2], ident[:])
+            t_bank["u", q, h] = bank
 
-        def empty_y(i):
-            y_turned[i] = work.tile([P, 2 * P * PACK], BF16, name="y_turned", align_bytes=256)
-            empty_pairs(y_turned[i], y_pair_bank[i])
-            release_bank(("y pairs", i))
+        def evac_u(q, h):
+            bank = t_bank["u", q, h]
+            u_t[q, h] = work.tile([P, 2 * GT], F32, name="u_t%d_%d" % (q, h), tag="u_t", bufs=8)
+            src = bank[:].rearrange("p w r -> p (w r)")
+            if ("u", q, h) in EVAC_V:
+                nc.vector.tensor_copy(out=u_t[q, h][:], in_=src)
+            else:
+                nc.scalar.copy(out=u_t[q, h][:], in_=src)
 
-        def quantize_y(i):
-            y_codes[i] = work.tile([P, Y_PASSES * P], U32, name="y_codes", bufs=3, align_bytes=256)
-            y_scales[i] = work.tile([P, Y_PASSES * P], U8, name="y_scales", bufs=3, align_bytes=256)
-            nc.vector.quantize_mx(out=y_codes[i][:].bitcast(FP8X4), scales=y_scales[i][:], in_=y_turned[i][:])
+        def mm1(q, h, w):
+            bank = psum.tile([P, 2, GT], F32, name="yb%d_%d_%d" % (q, h, w), tag="bank", bufs=8)
+            y_bank[q, h, w] = bank
+            for e in range(2):
+                t = 2 * w + e
+                cols = slice(t * P, (t + 1) * P)
+                for g in range(PASSES):
+                    nc.tensor.matmul_mx(out=bank[:, e, :], lhsT=c_code[h, g][:, cols].bitcast(FP8X4), lhsT_scale=c_sc[h, g][:, cols],
+                                        rhs=h_code[q, g][:].bitcast(FP8X4), rhs_scale=h_sc[q, g][:],
+                                        start=(g == 0), stop=(g == PASSES - 1))
 
-        def project(i, h):
-            o_banks[i, h] = take_bank(("o", i, h), [P, HALF])
-            for g in range(Y_PASSES):
-                tokens = slice(g * P, (g + 1) * P)
-                nc.tensor.matmul_mx(
-                    out=o_banks[i, h][:],
-                    lhsT=y_codes[i][:, tokens].bitcast(FP8X4),
-                    lhsT_scale=y_scales[i][:, tokens],
-                    rhs=w_words[:, g, 2 * h * HALF : 2 * (h + 1) * HALF].bitcast(FP4X4),
-                    rhs_scale=w_scales[:, g, half_cols(h)],
-                    start=(g == 0),
-                    stop=(g == Y_PASSES - 1),
-                )
+        def skip(q, h, w):
+            if w == 0:
+                y_pl[q, h] = work.tile([P, PACK, GT], BF16, name="y_pl%d_%d" % (q, h), tag="y_pl", bufs=4)
+            pairs = u_t[q, h][:].bitcast(BF16).rearrange("p (w r e) -> p w e r", w=2, e=2)
+            for e in range(2):
+                t = 2 * w + e
+                nc.vector.scalar_tensor_tensor(out=y_pl[q, h][:, t, :], in0=pairs[:, w, e, :], scalar=d_col[:, h, t:t + 1],
+                                               in1=y_bank[q, h, w][:, e, :], op0=ALU.mult, op1=ALU.add)
 
-        def sigmoid_cols(i, cols):
-            if i not in sig:
-                sig[i] = work.tile([P, R], F32, name="sig", bufs=4)
-            nc.scalar.activation(out=sig[i][:, cols], in_=gate_sb[:, i, cols], func=ACT.Sigmoid)
+        def weave_y(q, h):
+            y_in[q, h] = work.tile([P, GT * PACK], BF16, name="y_in%d_%d" % (q, h), tag="y_in", bufs=3, align_bytes=64)
+            dst = y_in[q, h][:].rearrange("p (c i t) -> p c t i", i=4, t=PACK)
+            src = y_pl[q, h][:].rearrange("p t (c i) -> p c t i", i=4)
+            if (q, h) in YIL_S:
+                nc.scalar.copy(out=dst, in_=src)
+            elif (q, h) in YIL_G:
+                nc.gpsimd.tensor_scalar(out=dst, in0=src, scalar1=1.0, scalar2=0.0, op0=ALU.mult, op1=ALU.add)
+            else:
+                nc.vector.tensor_copy(out=dst, in_=src)
 
-        def sigmoid(i):
-            sigmoid_cols(i, slice(GATE_FIRST if i == 0 else 0, R))
+        def quant_y(q, h):
+            y_code[q, h] = work.tile([P, GT], U32, name="y_code%d_%d" % (q, h), tag="y_code", bufs=8, align_bytes=64)
+            y_sc[q, h] = work.tile([P, GT], U8, name="y_sc%d_%d" % (q, h), tag="y_sc", bufs=8, align_bytes=64)
+            nc.vector.quantize_mx(out=y_code[q, h][:].bitcast(FP8X4), scales=y_sc[q, h][:], in_=y_in[q, h][:])
 
-        def apply_gate(i, h):
-            o_sb = work.tile([P, HALF], F32, name="o_sb", bufs=8)
-            nc.vector.tensor_tensor(out=o_sb[:], in0=o_banks[i, h][:], in1=sig[i][:, half_cols(h)], op=ALU.mult)
-            release_bank(("o", i, h))
-            nc.sync.dma_start(out=out_rows[:, i, half_cols(h)], in_=o_sb[:])
+        def sigmoid(j):
+            sig[j] = work.tile([P, R], F32, name="sig%d" % j, tag="sig", bufs=6)
+            q, i = divmod(j, PAIR)
+            nc.scalar.activation(out=sig[j][:], in_=g_raw[q][:, i * R:(i + 1) * R], func=ACT.Sigmoid)
 
-        stage = {
-            "widen": widen,
-            "turn_h": turn_h,
-            "empty_h": empty_h,
-            "quantize_h": quantize_h,
-            "group_c": group_c,
-            "quantize_c": quantize_c,
-            "skip_term": skip_term,
-            "add_skip": add_skip,
-            "turn_y": turn_y,
-            "empty_y": empty_y,
-            "quantize_y": quantize_y,
-            "sigmoid": sigmoid,
-            "project": project,
-            "apply_gate": apply_gate,
-        }
+        def mm2(j, s, h):
+            q, i = divmod(j, PAIR)
+            if h == 0:
+                o_bank[j, s] = psum.tile([P, KP], F32, name="ob%d_%d" % (j, s), tag="bank", bufs=8)
+            cols = slice(i * P, (i + 1) * P)
+            nc.tensor.matmul_mx(out=o_bank[j, s][:], lhsT=y_code[q, h][:, cols].bitcast(FP8X4), lhsT_scale=y_sc[q, h][:, cols],
+                                rhs=w_words[:, h, 2 * KP * s:2 * KP * (s + 1)].bitcast(FP4X4), rhs_scale=w_scale[:, h, KP * s:KP * (s + 1)],
+                                start=(h == 0), stop=(h == HALVES - 1))
 
-        def index_at(name, step, delay):
-            index = step - delay
-            if name in H_STAGES and index < EARLY_TILES:
-                index += EARLY_STEPS
-                return index if 0 <= index < EARLY_TILES else None
-            return index if 0 <= index < (H_PASSES if name in C_STAGES else TILES) else None
+        def finish(j, s):
+            part = sig[j][:, KP * s:KP * (s + 1)]
+            nc.vector.tensor_tensor(out=part, in0=o_bank[j, s][:], in1=part, op=ALU.mult)
+            nc.sync.dma_start(out=o_rows[:, j, KP * s:KP * (s + 1)], in_=part)
 
-        sigmoid_cols(0, slice(0, GATE_FIRST))
-        for step in range(STEPS):
-            if step == SPREAD_D_STEP:
-                spread_d()
-            for name, part, delay in STAGES:
-                if name == "readout":
-                    readout(part)
-                    continue
-                index = index_at(name, step, delay)
-                if index is None:
-                    continue
-                if part is None:
-                    stage[name](index)
-                else:
-                    stage[name](index, part)
+        nc.sync.dma_start(out=h_scale[:], in_=H_scale.rearrange("(p j) b -> p (j b)", j=TILES))
+        load_h(0)
+        load_h(1)
+        load_h(2)
+        load_h(3)
+        load_c(0, 0)
+        load_h(4)
+        load_h(5)
+        load_c(0, 1)
+        load_c(0, 2)
+        load_u(0)
+        load_c(0, 3)
+        load_h(6)
+        load_h(7)
+        load_u(1)
+        nc.sync.dma_start(out=d_col[:], in_=d.rearrange("(h p t) -> p h t", p=P, t=PACK))
+        load_c(1, 0)
+        load_u(2)
+        load_c(1, 1)
+        load_u(3)
+        load_c(1, 2)
+        load_c(1, 3)
+        load_g(0)
+        load_w()
+        load_g(1)
+        load_g(2)
+        load_g(3)
+        widen(1, [0])
+        widen(0, [0])
+        turn_h(0,0)
+        widen(0, [1])
+        widen(1, [1])
+        widen(0, [2])
+        widen(0, [3])
+        widen(1, [2])
+        turn_h(0,1)
+        widen(2, [0])
+        widen(2, [1])
+        widen(1, [3])
+        turn_h(0,2)
+        widen(2, [2])
+        widen(2, [3])
+        evac_h(0,0)
+        turn_h(0,3)
+        widen(3, [0])
+        widen(3, [1])
+        evac_h(0,1)
+        pweave_c(0,0,0)
+        widen(3, [2])
+        evac_h(0,2)
+        pweave_c(0,0,1)
+        widen(3, [3])
+        widen(4, [0])
+        evac_h(0,3)
+        turn_h(1,0)
+        widen(4, [1])
+        turn_h(1,1)
+        evac_c(0,0,0)
+        widen(4, [2])
+        turn_h(1,2)
+        widen(4, [3])
+        evac_c(0,0,1)
+        turn_h(1,3)
+        quant_h(0,0)
+        pweave_c(0,1,0)
+        quant_h(0,1)
+        evac_h(1,0)
+        quant_h(0,2)
+        pweave_c(0,1,1)
+        quant_h(0,3)
+        evac_h(1,1)
+        widen(5, [0])
+        turn_h(2,0)
+        evac_h(1,2)
+        widen(5, [1])
+        widen(5, [2])
+        evac_h(1,3)
+        turn_h(2,1)
+        widen(5, [3])
+        turn_h(2,2)
+        quant_c(0,0)
+        evac_c(0,1,0)
+        turn_h(2,3)
+        quant_h(1,0)
+        evac_c(0,1,1)
+        pweave_c(0,2,0)
+        quant_h(1,1)
+        evac_h(2,0)
+        quant_h(1,2)
+        pweave_c(0,2,1)
+        quant_h(1,3)
+        evac_h(2,1)
+        quant_c(0,1)
+        turn_u(0,0)
+        evac_h(2,2)
+        pweave_c(0,3,0)
+        widen(6, [0])
+        widen(6, [1])
+        evac_h(2,3)
+        pweave_c(0,3,1)
+        widen(6, [2])
+        evac_c(0,2,0)
+        widen(6, [3])
+        turn_u(0,1)
+        widen(7, [0])
+        evac_c(0,2,1)
+        turn_u(1,0)
+        widen(7, [1])
+        widen(7, [2])
+        evac_c(0,3,0)
+        turn_h(3,0)
+        widen(7, [3])
+        turn_h(3,1)
+        evac_c(0,3,1)
+        quant_h(2,0)
+        turn_h(3,2)
+        quant_h(2,1)
+        evac_h(3,0)
+        quant_h(2,2)
+        quant_h(2,3)
+        evac_h(3,1)
+        quant_c(0,2)
+        evac_h(3,2)
+        evac_u(0,0)
+        turn_h(3,3)
+        turn_u(1,1)
+        evac_h(3,3)
+        quant_c(0,3)
+        mm1(0,0,0)
+        evac_u(1,1)
+        evac_u(0,1)
+        weave_c(1,1)
+        evac_u(1,0)
+        weave_c(1,0)
+        mm1(0,0,1)
+        skip(0,0,0)
+        turn_u(2,0)
+        evac_u(2,0)
+        quant_c(1,0)
+        turn_u(2,1)
+        skip(0,0,1)
+        mm1(1,0,0)
+        evac_u(2,1)
+        quant_h(3,0)
+        weave_c(1,3)
+        quant_h(3,1)
+        mm1(1,0,1)
+        quant_h(3,2)
+        quant_h(3,3)
+        weave_c(1,2)
+        turn_u(3,0)
+        turn_u(3,1)
+        skip(1,0,0)
+        mm1(2,0,0)
+        evac_u(3,0)
+        quant_c(1,1)
+        evac_u(3,1)
+        skip(1,0,1)
+        mm1(2,0,1)
+        weave_y(0,0)
+        quant_c(1,2)
+        skip(2,0,0)
+        mm1(3,0,0)
+        weave_y(1,0)
+        quant_c(1,3)
+        skip(2,0,1)
+        mm1(3,0,1)
+        weave_y(2,0)
+        quant_y(0,0)
+        skip(3,0,0)
+        mm1(0,1,0)
+        quant_y(1,0)
+        skip(3,0,1)
+        sigmoid(0)
+        mm1(0,1,1)
+        skip(0,1,0)
+        quant_y(2,0)
+        sigmoid(1)
+        mm1(1,1,0)
+        skip(0,1,1)
+        weave_y(0,1)
+        mm1(1,1,1)
+        skip(1,1,0)
+        mm2(0,0,0)
+        quant_y(0,1)
+        mm2(0,0,1)
+        skip(1,1,1)
+        weave_y(1,1)
+        finish(0,0)
+        mm2(0,1,0)
+        mm2(0,1,1)
+        mm1(2,1,0)
+        finish(0,1)
+        weave_y(3,0)
+        skip(2,1,0)
+        mm2(1,0,0)
+        mm2(1,0,1)
+        sigmoid(2)
+        mm2(1,1,0)
+        quant_y(1,1)
+        mm2(1,1,1)
+        finish(1,0)
+        mm1(2,1,1)
+        finish(1,1)
+        sigmoid(3)
+        skip(2,1,1)
+        mm2(2,0,0)
+        weave_y(2,1)
+        mm2(2,0,1)
+        mm2(2,1,0)
+        quant_y(3,0)
+        mm2(2,1,1)
+        finish(2,0)
+        mm1(3,1,0)
+        finish(2,1)
+        sigmoid(4)
+        skip(3,1,0)
+        mm2(3,0,0)
+        mm2(3,0,1)
+        sigmoid(5)
+        mm2(3,1,0)
+        quant_y(2,1)
+        mm2(3,1,1)
+        finish(3,0)
+        mm1(3,1,1)
+        finish(3,1)
+        sigmoid(6)
+        skip(3,1,1)
+        mm2(4,0,0)
+        sigmoid(7)
+        mm2(4,0,1)
+        mm2(4,1,0)
+        finish(4,0)
+        mm2(4,1,1)
+        weave_y(3,1)
+        mm2(5,0,0)
+        mm2(5,0,1)
+        finish(4,1)
+        mm2(5,1,0)
+        mm2(5,1,1)
+        quant_y(3,1)
+        finish(5,0)
+        mm2(6,0,0)
+        mm2(6,1,0)
+        finish(5,1)
+        mm2(7,0,0)
+        mm2(7,1,0)
+        mm2(6,0,1)
+        finish(6,0)
+        mm2(6,1,1)
+        mm2(7,0,1)
+        mm2(7,1,1)
+        finish(6,1)
+        finish(7,0)
+        finish(7,1)

@@ -20,21 +20,24 @@ ACT = mybir.ActivationFunctionType
 P = 128
 PACK = 4
 KP = P * PACK
+WORDS = KP // 2
 TILES = T // P
 PAIR = 2
 GT = PAIR * P
 GROUPS = TILES // PAIR
 PASSES = K // KP
 HALVES = N // KP
+BANK = 512
+SPANS = R // BANK
 BLK = 128
+BLOCKS = K // BLK
 
-EVAC_V = (("u", 0, 0), ("u", 0, 1), ("u", 1, 0),)
-YIL_G = ()
-LAG = 3
-TB, YB, OB = 2, 3, 3
-WIDEN_S = (1,)
-CIL_V = ((1, 0), (1, 2),)
-YIL_S = ((0, 0), (1, 0), (2, 0), (1, 1), (3, 0), (2, 1),)
+WIDEN_ON_SCALAR = (1, 5)
+WEAVE_ON_SCALAR = ((1, 1), (1, 3))
+
+OUT_LAG = 4
+QUANT_LAG = 2
+EARLY_GATES = 2
 
 
 def tile_state_space_readout_d4_kernel(tc, H_bytes, H_scale, C, u, d, W_words, W_scales, gate, out):
@@ -42,456 +45,234 @@ def tile_state_space_readout_d4_kernel(tc, H_bytes, H_scale, C, u, d, W_words, W
     with ExitStack() as ctx:
         keep = ctx.enter_context(tc.tile_pool(name="keep", bufs=1))
         work = ctx.enter_context(tc.tile_pool(name="work", bufs=2))
-        psum = ctx.enter_context(tc.psum_pool(name="psum", bufs=1))
+        psum = ctx.enter_context(tc.psum_pool(name="psum", bufs=8))
         ctx.enter_context(tc.manual_schedule())
 
         h_rows = H_bytes.rearrange("(p j) k -> p j k", j=TILES)
-        u_rows = u.rearrange("(p j) n -> p j n", j=TILES)
-        g_rows = gate.rearrange("(p j) r -> p j r", j=TILES)
-        o_rows = out.rearrange("(p j) r -> p j r", j=TILES)
+        u_rows = u.rearrange("(p j) n -> p (j n)", j=TILES)
+        gate_rows = gate.rearrange("(p j) r -> p (j r)", j=TILES)
+        out_rows = out.rearrange("(p j) r -> p j r", j=TILES)
 
         ident = keep.tile([P, P], F32, name="ident")
         w_scale = keep.tile([P, HALVES, R], U8, name="w_scale", align_bytes=64)
-        warm = keep.tile([P, 2], F32, name="warm")
+        table_probe = keep.tile([P, 2], F32, name="table_probe")
         make_identity(nc, ident[:])
-        nc.scalar.activation(out=warm[:], in_=ident[:, 0:2], func=ACT.Sigmoid)
-        ident16 = keep.tile([P, P], BF16, name="ident16")
-        make_identity(nc, ident16[:])
+        nc.scalar.activation(out=table_probe[:], in_=ident[:, 0:2], func=ACT.Sigmoid)
         nc.gpsimd.memset(w_scale[:].rearrange("p h r -> p (h r)").bitcast(I32), 0)
 
-        h_scale = keep.tile([P, TILES * K // BLK], F32, name="h_scale")
+        h_scale = keep.tile([P, TILES * BLOCKS], F32, name="h_scale")
         d_col = keep.tile([P, HALVES, PACK], BF16, name="d_col")
         w_words = keep.tile([P, HALVES, 2 * R], U8, name="w_words", align_bytes=64)
-        h_raw, c_raw, u_raw, g_raw = {}, {}, {}, {}
-        h_wide, h_in, h_code, h_sc, c_in, c_code, c_sc = {}, {}, {}, {}, {}, {}, {}
-        t_bank = {}
-        u_t, y_bank, y_pl, y_in, y_code, y_sc, sig, o_bank, res = {}, {}, {}, {}, {}, {}, {}, {}, {}
+        h_raw, c_raw, u_raw, gate_raw = {}, {}, {}, {}
+        h_wide, h_woven, h_code, h_exp = {}, {}, {}, {}
+        c_woven, c_code, c_exp = {}, {}, {}
+        u_bank, u_turned = {}, {}
+        y_bank, y_planes, y_woven, y_code, y_exp = {}, {}, {}, {}, {}
+        gated, out_bank = {}, {}
 
         def load_h(j):
             h_raw[j] = keep.tile([P, K], U8, name="h_raw%d" % j)
             nc.sync.dma_start(out=h_raw[j][:], in_=h_rows[:, j, :])
 
         def load_c(h, g):
-            c_raw[h, g] = keep.tile([P, PACK, KP], BF16, name="c_raw%d_%d" % (h, g))
+            c_raw[h, g] = work.tile([P, PACK, KP], BF16, name="c_raw%d_%d" % (h, g), tag="c_raw", bufs=5)
             rows = C[g * KP:(g + 1) * KP, h * KP:(h + 1) * KP]
-            nc.sync.dma_start(out=c_raw[h, g][:], in_=rows.rearrange("(p j) n -> p j n", j=PACK))
+            nc.sync.dma_start(out=c_raw[h, g][:], in_=rows.rearrange("(p t) n -> p t n", t=PACK))
 
-        def load_u(q):
-            u_raw[q] = work.tile([P, PAIR * N], BF16, name="u_raw%d" % q, tag="rows", bufs=8)
-            nc.sync.dma_start(out=u_raw[q][:], in_=u_rows[:, PAIR * q:PAIR * (q + 1), :].rearrange("p j n -> p (j n)"))
-
-        def load_g(q):
-            g_raw[q] = work.tile([P, PAIR * R], BF16, name="g_raw%d" % q, tag="rows", bufs=8)
-            nc.sync.dma_start(out=g_raw[q][:], in_=g_rows[:, PAIR * q:PAIR * (q + 1), :].rearrange("p j n -> p (j n)"))
+        def load_rows(tiles, rows, q, label):
+            tiles[q] = work.tile([P, PAIR * N], BF16, name="%s%d" % (label, q), tag="rows", bufs=5)
+            nc.sync.dma_start(out=tiles[q][:], in_=rows[:, q * PAIR * N:(q + 1) * PAIR * N])
 
         def load_w():
             nc.sync.dma_start(out=w_words[:], in_=W_words.rearrange("h p b -> p h b"))
             for quad in range(4):
                 nc.sync.dma_start(
                     out=w_scale[32 * quad:32 * quad + 4, :, :].bitcast(I32),
-                    in_=W_scales[:, 4 * quad:4 * quad + 4, :].rearrange("h q r -> q h r").bitcast(I32),
+                    in_=W_scales[:, 4 * quad:4 * quad + 4, :].rearrange("h i r -> i h r").bitcast(I32),
                 )
 
-        def widen(j, gs=range(PASSES)):
-            if j not in h_wide:
-                h_wide[j] = work.tile([P, K], BF16, name="h_wide%d" % j, tag="h_wide", bufs=4)
-            for g in gs:
-                for b in range(KP // BLK):
-                    blk = g * (KP // BLK) + b
-                    src = h_raw[j][:, blk * BLK:(blk + 1) * BLK].bitcast(FP8)
-                    col = j * (K // BLK) + blk
-                    if j in WIDEN_S:
-                        nc.scalar.activation(out=h_wide[j][:, blk * BLK:(blk + 1) * BLK], in_=src, func=ACT.Copy,
-                                             scale=h_scale[:, col:col + 1])
-                    else:
-                        dst = h_wide[j][:, g * KP:(g + 1) * KP].rearrange("p (w m e) -> p m w e", w=2, e=2)
-                        nc.vector.tensor_scalar(out=dst[:, 32 * b:32 * (b + 1), :, :], in0=src.rearrange("p (m w e) -> p m w e", w=2, e=2),
-                                                scalar1=h_scale[:, col:col + 1], scalar2=None, op0=ALU.mult)
+        def widen(j):
+            h_wide[j] = work.tile([P, K], BF16, name="h_wide%d" % j, tag="wide", bufs=TILES)
+            for b in range(BLOCKS):
+                cols = slice(b * BLK, (b + 1) * BLK)
+                scale = h_scale[:, j * BLOCKS + b:j * BLOCKS + b + 1]
+                codes = h_raw[j][:, cols].bitcast(FP8)
+                if j in WIDEN_ON_SCALAR:
+                    nc.scalar.activation(out=h_wide[j][:, cols], in_=codes, func=ACT.Copy, scale=scale)
+                else:
+                    nc.vector.tensor_scalar(out=h_wide[j][:, cols], in0=codes, scalar1=scale, scalar2=None, op0=ALU.mult)
+
+        def turn(name, words_of_tile):
+            bank = psum.tile([P, 2, GT], F32, name=name, tag="bank")
+            for i in range(PAIR):
+                for w in range(2):
+                    nc.tensor.transpose(bank[:, w, i * P:(i + 1) * P], words_of_tile(i)[:, w:WORDS:2], ident[:])
+            return bank
 
         def turn_h(q, g):
-            bank = psum.tile([P, 2, GT], F32, name="tb_h%d_%d" % (q, g), tag="bank", bufs=8)
-            for i in range(PAIR):
-                j = PAIR * q + i
-                words = h_wide[j][:].bitcast(F32)
-                for w in range(2):
-                    if j in WIDEN_S:
-                        src = words[:, 256 * g + w:256 * (g + 1):2]
-                    else:
-                        src = words[:, 256 * g + 128 * w:256 * g + 128 * (w + 1)]
-                    nc.tensor.transpose(bank[:, w, i * P:(i + 1) * P], src, ident[:])
-            t_bank["h", q, g] = bank
+            bank = turn("h_bank%d_%d" % (q, g), lambda i: h_wide[PAIR * q + i][:, g * KP:(g + 1) * KP].bitcast(F32))
+            h_woven[q, g] = work.tile([P, GT * PACK], BF16, name="h_woven%d_%d" % (q, g), tag="h_woven", bufs=12, align_bytes=64)
+            nc.scalar.copy(
+                out=h_woven[q, g][:].bitcast(F32).rearrange("p (r w) -> p r w", w=2),
+                in_=bank[:].rearrange("p w r -> p r w"),
+            )
 
-        def evac_h(q, g):
-            bank = t_bank["h", q, g]
-            h_in[q, g] = work.tile([P, GT * PACK], BF16, name="h_in%d_%d" % (q, g), tag="h_in", bufs=6, align_bytes=64)
-            dst = h_in[q, g][:].bitcast(F32).rearrange("p (r w) -> p r w", w=2)
-            src = bank[:].rearrange("p w r -> p r w")
-            if ("h", q, g) in EVAC_V:
-                nc.vector.tensor_copy(out=dst, in_=src)
-            else:
-                nc.scalar.copy(out=dst, in_=src)
+        def quantize(name, woven):
+            columns = woven[:].shape[1] // PACK
+            code = keep.tile([P, columns], U32, name=name + "_code", align_bytes=64)
+            exp = keep.tile([P, columns], U8, name=name + "_exp", align_bytes=64)
+            nc.vector.quantize_mx(out=code[:].bitcast(FP8X4), scales=exp[:], in_=woven[:])
+            return code, exp
 
-        def quant_h(q, g):
-            h_code[q, g] = keep.tile([P, GT], U32, name="h_code%d_%d" % (q, g), align_bytes=64)
-            h_sc[q, g] = keep.tile([P, GT], U8, name="h_sc%d_%d" % (q, g), align_bytes=64)
-            nc.vector.quantize_mx(out=h_code[q, g][:].bitcast(FP8X4), scales=h_sc[q, g][:], in_=h_in[q, g][:])
+        def quant_h(q):
+            for g in range(PASSES):
+                h_code[q, g], h_exp[q, g] = quantize("h%d_%d" % (q, g), h_woven[q, g])
 
         def weave_c(h, g):
-            c_in[h, g] = work.tile([P, KP * PACK], BF16, name="c_in%d_%d" % (h, g), tag="c_in", bufs=4, align_bytes=64)
-            dst = c_in[h, g][:].rearrange("p (t m j) -> p m j t", t=PACK, j=PACK)
-            src = c_raw[h, g][:].rearrange("p j (m t) -> p m j t", t=PACK)
-            if (h, g) in CIL_V:
-                nc.vector.tensor_copy(out=dst, in_=src)
-            else:
+            c_woven[h, g] = work.tile([P, KP * PACK], BF16, name="c_woven%d_%d" % (h, g), tag="c_woven", bufs=4, align_bytes=64)
+            dst = c_woven[h, g][:].rearrange("p (t m row) -> p m row t", t=PACK, row=PACK)
+            src = c_raw[h, g][:].rearrange("p row (m t) -> p m row t", t=PACK)
+            if (h, g) in WEAVE_ON_SCALAR:
                 nc.scalar.copy(out=dst, in_=src)
-
-        def pweave_c(h, g, w):
-            bank = psum.tile([P, 2, KP], BF16, name="cb%d_%d_%d" % (h, g, w), tag="bank", bufs=8)
-            t_bank["c", h, g, w] = bank
-            src = c_raw[h, g][:].rearrange("p j (m t) -> p t m j", t=PACK)
-            for e in range(2):
-                nc.tensor.matmul(out=bank[:, e, :], lhsT=ident16[:], rhs=src[:, 2 * w + e, :, :], start=True, stop=True)
-
-        def evac_c(h, g, w):
-            if w == 0:
-                c_in[h, g] = work.tile([P, KP * PACK], BF16, name="c_in%d_%d" % (h, g), tag="c_in", bufs=4, align_bytes=64)
-            dst = c_in[h, g][:, 2 * KP * w:2 * KP * (w + 1)]
-            src = t_bank["c", h, g, w][:].rearrange("p e n -> p (e n)")
-            if ("c", h, g, w) in EVAC_V:
-                nc.vector.tensor_copy(out=dst, in_=src)
             else:
-                nc.scalar.copy(out=dst, in_=src)
+                nc.vector.tensor_copy(out=dst, in_=src)
 
         def quant_c(h, g):
-            c_code[h, g] = keep.tile([P, KP], U32, name="c_code%d_%d" % (h, g), align_bytes=64)
-            c_sc[h, g] = keep.tile([P, KP], U8, name="c_sc%d_%d" % (h, g), align_bytes=64)
-            nc.vector.quantize_mx(out=c_code[h, g][:].bitcast(FP8X4), scales=c_sc[h, g][:], in_=c_in[h, g][:])
+            c_code[h, g], c_exp[h, g] = quantize("c%d_%d" % (h, g), c_woven[h, g])
 
         def turn_u(q, h):
-            bank = psum.tile([P, 2, GT], F32, name="tb_u%d_%d" % (q, h), tag="bank", bufs=8)
-            words = u_raw[q][:].bitcast(F32)
-            for i in range(PAIR):
-                for w in range(2):
-                    base = i * (N // 2) + 256 * h
-                    nc.tensor.transpose(bank[:, w, i * P:(i + 1) * P], words[:, base + w:base + 256:2], ident[:])
-            t_bank["u", q, h] = bank
+            u_bank[q, h] = turn("u_bank%d_%d" % (q, h), lambda i: u_raw[q][:, i * N + h * KP:i * N + (h + 1) * KP].bitcast(F32))
 
-        def evac_u(q, h):
-            bank = t_bank["u", q, h]
-            u_t[q, h] = work.tile([P, 2 * GT], F32, name="u_t%d_%d" % (q, h), tag="u_t", bufs=8)
-            src = bank[:].rearrange("p w r -> p (w r)")
-            if ("u", q, h) in EVAC_V:
-                nc.vector.tensor_copy(out=u_t[q, h][:], in_=src)
-            else:
-                nc.scalar.copy(out=u_t[q, h][:], in_=src)
+        def empty_u(q, h):
+            u_turned[q, h] = keep.tile([P, 2 * GT], F32, name="u_turned%d_%d" % (q, h))
+            nc.scalar.copy(out=u_turned[q, h][:], in_=u_bank[q, h][:].rearrange("p w r -> p (w r)"))
 
-        def mm1(q, h, w):
-            bank = psum.tile([P, 2, GT], F32, name="yb%d_%d_%d" % (q, h, w), tag="bank", bufs=8)
-            y_bank[q, h, w] = bank
+        def readout(q, h, w):
+            y_bank[q, h, w] = psum.tile([P, 2, GT], F32, name="y_bank%d_%d_%d" % (q, h, w), tag="bank")
             for e in range(2):
-                t = 2 * w + e
-                cols = slice(t * P, (t + 1) * P)
+                cols = slice((2 * w + e) * P, (2 * w + e + 1) * P)
                 for g in range(PASSES):
-                    nc.tensor.matmul_mx(out=bank[:, e, :], lhsT=c_code[h, g][:, cols].bitcast(FP8X4), lhsT_scale=c_sc[h, g][:, cols],
-                                        rhs=h_code[q, g][:].bitcast(FP8X4), rhs_scale=h_sc[q, g][:],
-                                        start=(g == 0), stop=(g == PASSES - 1))
+                    nc.tensor.matmul_mx(
+                        out=y_bank[q, h, w][:, e, :],
+                        lhsT=c_code[h, g][:, cols].bitcast(FP8X4), lhsT_scale=c_exp[h, g][:, cols],
+                        rhs=h_code[q, g][:].bitcast(FP8X4), rhs_scale=h_exp[q, g][:],
+                        start=(g == 0), stop=(g == PASSES - 1),
+                    )
 
-        def skip(q, h, w):
+        def add_skip(q, h, w):
             if w == 0:
-                y_pl[q, h] = work.tile([P, PACK, GT], BF16, name="y_pl%d_%d" % (q, h), tag="y_pl", bufs=4)
-            pairs = u_t[q, h][:].bitcast(BF16).rearrange("p (w r e) -> p w e r", w=2, e=2)
+                y_planes[q, h] = work.tile([P, PACK, GT], BF16, name="y_planes%d_%d" % (q, h), tag="y_planes", bufs=6)
+            u_planes = u_turned[q, h][:].bitcast(BF16).rearrange("p (w r e) -> p w e r", w=2, e=2)
             for e in range(2):
                 t = 2 * w + e
-                nc.vector.scalar_tensor_tensor(out=y_pl[q, h][:, t, :], in0=pairs[:, w, e, :], scalar=d_col[:, h, t:t + 1],
-                                               in1=y_bank[q, h, w][:, e, :], op0=ALU.mult, op1=ALU.add)
+                nc.vector.scalar_tensor_tensor(
+                    out=y_planes[q, h][:, t, :], in0=u_planes[:, w, e, :], scalar=d_col[:, h, t:t + 1],
+                    in1=y_bank[q, h, w][:, e, :], op0=ALU.mult, op1=ALU.add,
+                )
 
         def weave_y(q, h):
-            y_in[q, h] = work.tile([P, GT * PACK], BF16, name="y_in%d_%d" % (q, h), tag="y_in", bufs=3, align_bytes=64)
-            dst = y_in[q, h][:].rearrange("p (c i t) -> p c t i", i=4, t=PACK)
-            src = y_pl[q, h][:].rearrange("p t (c i) -> p c t i", i=4)
-            if (q, h) in YIL_S:
-                nc.scalar.copy(out=dst, in_=src)
-            elif (q, h) in YIL_G:
-                nc.gpsimd.tensor_scalar(out=dst, in0=src, scalar1=1.0, scalar2=0.0, op0=ALU.mult, op1=ALU.add)
-            else:
-                nc.vector.tensor_copy(out=dst, in_=src)
+            y_woven[q, h] = work.tile([P, GT * PACK], BF16, name="y_woven%d_%d" % (q, h), tag="y_woven", bufs=6, align_bytes=64)
+            nc.scalar.copy(
+                out=y_woven[q, h][:].rearrange("p (c i t) -> p c t i", i=4, t=PACK),
+                in_=y_planes[q, h][:].rearrange("p t (c i) -> p c t i", i=4),
+            )
 
         def quant_y(q, h):
-            y_code[q, h] = work.tile([P, GT], U32, name="y_code%d_%d" % (q, h), tag="y_code", bufs=8, align_bytes=64)
-            y_sc[q, h] = work.tile([P, GT], U8, name="y_sc%d_%d" % (q, h), tag="y_sc", bufs=8, align_bytes=64)
-            nc.vector.quantize_mx(out=y_code[q, h][:].bitcast(FP8X4), scales=y_sc[q, h][:], in_=y_in[q, h][:])
+            y_code[q, h], y_exp[q, h] = quantize("y%d_%d" % (q, h), y_woven[q, h])
 
         def sigmoid(j):
-            sig[j] = work.tile([P, R], F32, name="sig%d" % j, tag="sig", bufs=6)
+            gated[j] = work.tile([P, R], F32, name="gated%d" % j, tag="wide", bufs=TILES)
             q, i = divmod(j, PAIR)
-            nc.scalar.activation(out=sig[j][:], in_=g_raw[q][:, i * R:(i + 1) * R], func=ACT.Sigmoid)
+            nc.scalar.activation(out=gated[j][:], in_=gate_raw[q][:, i * R:(i + 1) * R], func=ACT.Sigmoid)
 
-        def mm2(j, s, h):
+        def project(j):
             q, i = divmod(j, PAIR)
-            if h == 0:
-                o_bank[j, s] = psum.tile([P, KP], F32, name="ob%d_%d" % (j, s), tag="bank", bufs=8)
-            cols = slice(i * P, (i + 1) * P)
-            nc.tensor.matmul_mx(out=o_bank[j, s][:], lhsT=y_code[q, h][:, cols].bitcast(FP8X4), lhsT_scale=y_sc[q, h][:, cols],
-                                rhs=w_words[:, h, 2 * KP * s:2 * KP * (s + 1)].bitcast(FP4X4), rhs_scale=w_scale[:, h, KP * s:KP * (s + 1)],
-                                start=(h == 0), stop=(h == HALVES - 1))
+            tokens = slice(i * P, (i + 1) * P)
+            for h in range(HALVES):
+                for s in range(SPANS):
+                    if h == 0:
+                        out_bank[j, s] = psum.tile([P, BANK], F32, name="out_bank%d_%d" % (j, s), tag="bank")
+                    nc.tensor.matmul_mx(
+                        out=out_bank[j, s][:],
+                        lhsT=y_code[q, h][:, tokens].bitcast(FP8X4), lhsT_scale=y_exp[q, h][:, tokens],
+                        rhs=w_words[:, h, 2 * BANK * s:2 * BANK * (s + 1)].bitcast(FP4X4),
+                        rhs_scale=w_scale[:, h, BANK * s:BANK * (s + 1)],
+                        start=(h == 0), stop=(h == HALVES - 1),
+                    )
 
-        def finish(j, s):
-            part = sig[j][:, KP * s:KP * (s + 1)]
-            nc.vector.tensor_tensor(out=part, in0=o_bank[j, s][:], in1=part, op=ALU.mult)
-            nc.sync.dma_start(out=o_rows[:, j, KP * s:KP * (s + 1)], in_=part)
+        def finish(j):
+            for s in range(SPANS):
+                part = gated[j][:, BANK * s:BANK * (s + 1)]
+                nc.vector.tensor_tensor(out=part, in0=out_bank[j, s][:], in1=part, op=ALU.mult)
+                nc.sync.dma_start(out=out_rows[:, j, BANK * s:BANK * (s + 1)], in_=part)
 
         nc.sync.dma_start(out=h_scale[:], in_=H_scale.rearrange("(p j) b -> p (j b)", j=TILES))
-        load_h(0)
-        load_h(1)
-        load_h(2)
-        load_h(3)
-        load_c(0, 0)
-        load_h(4)
-        load_h(5)
-        load_c(0, 1)
-        load_c(0, 2)
-        load_u(0)
-        load_c(0, 3)
-        load_h(6)
-        load_h(7)
-        load_u(1)
+        for j in range(TILES):
+            load_h(j)
+        for g in range(PASSES):
+            load_c(0, g)
+            load_rows(u_raw, u_rows, g, "u_raw")
         nc.sync.dma_start(out=d_col[:], in_=d.rearrange("(h p t) -> p h t", p=P, t=PACK))
         load_c(1, 0)
-        load_u(2)
-        load_c(1, 1)
-        load_u(3)
-        load_c(1, 2)
-        load_c(1, 3)
-        load_g(0)
+
+        for j in range(TILES):
+            widen(j)
+        for step in range(GROUPS):
+            for g in range(PASSES):
+                turn_h(step, g)
+            weave_c(0, step)
+            if step + 1 < PASSES:
+                load_c(1, step + 1)
+            if step == 0:
+                quant_h(0)
+            else:
+                quant_c(0, step - 1)
+        quant_c(0, PASSES - 1)
+        for h in range(HALVES):
+            for q in range(GROUPS):
+                turn_u(q, h)
+        load_rows(gate_raw, gate_rows, 0, "gate_raw")
         load_w()
-        load_g(1)
-        load_g(2)
-        load_g(3)
-        widen(1, [0])
-        widen(0, [0])
-        turn_h(0,0)
-        widen(0, [1])
-        widen(1, [1])
-        widen(0, [2])
-        widen(0, [3])
-        widen(1, [2])
-        turn_h(0,1)
-        widen(2, [0])
-        widen(2, [1])
-        widen(1, [3])
-        turn_h(0,2)
-        widen(2, [2])
-        widen(2, [3])
-        evac_h(0,0)
-        turn_h(0,3)
-        widen(3, [0])
-        widen(3, [1])
-        evac_h(0,1)
-        pweave_c(0,0,0)
-        widen(3, [2])
-        evac_h(0,2)
-        pweave_c(0,0,1)
-        widen(3, [3])
-        widen(4, [0])
-        evac_h(0,3)
-        turn_h(1,0)
-        widen(4, [1])
-        turn_h(1,1)
-        evac_c(0,0,0)
-        widen(4, [2])
-        turn_h(1,2)
-        widen(4, [3])
-        evac_c(0,0,1)
-        turn_h(1,3)
-        quant_h(0,0)
-        pweave_c(0,1,0)
-        quant_h(0,1)
-        evac_h(1,0)
-        quant_h(0,2)
-        pweave_c(0,1,1)
-        quant_h(0,3)
-        evac_h(1,1)
-        widen(5, [0])
-        turn_h(2,0)
-        evac_h(1,2)
-        widen(5, [1])
-        widen(5, [2])
-        evac_h(1,3)
-        turn_h(2,1)
-        widen(5, [3])
-        turn_h(2,2)
-        quant_c(0,0)
-        evac_c(0,1,0)
-        turn_h(2,3)
-        quant_h(1,0)
-        evac_c(0,1,1)
-        pweave_c(0,2,0)
-        quant_h(1,1)
-        evac_h(2,0)
-        quant_h(1,2)
-        pweave_c(0,2,1)
-        quant_h(1,3)
-        evac_h(2,1)
-        quant_c(0,1)
-        turn_u(0,0)
-        evac_h(2,2)
-        pweave_c(0,3,0)
-        widen(6, [0])
-        widen(6, [1])
-        evac_h(2,3)
-        pweave_c(0,3,1)
-        widen(6, [2])
-        evac_c(0,2,0)
-        widen(6, [3])
-        turn_u(0,1)
-        widen(7, [0])
-        evac_c(0,2,1)
-        turn_u(1,0)
-        widen(7, [1])
-        widen(7, [2])
-        evac_c(0,3,0)
-        turn_h(3,0)
-        widen(7, [3])
-        turn_h(3,1)
-        evac_c(0,3,1)
-        quant_h(2,0)
-        turn_h(3,2)
-        quant_h(2,1)
-        evac_h(3,0)
-        quant_h(2,2)
-        quant_h(2,3)
-        evac_h(3,1)
-        quant_c(0,2)
-        evac_h(3,2)
-        evac_u(0,0)
-        turn_h(3,3)
-        turn_u(1,1)
-        evac_h(3,3)
-        quant_c(0,3)
-        mm1(0,0,0)
-        evac_u(1,1)
-        evac_u(0,1)
-        weave_c(1,1)
-        evac_u(1,0)
-        weave_c(1,0)
-        mm1(0,0,1)
-        skip(0,0,0)
-        turn_u(2,0)
-        evac_u(2,0)
-        quant_c(1,0)
-        turn_u(2,1)
-        skip(0,0,1)
-        mm1(1,0,0)
-        evac_u(2,1)
-        quant_h(3,0)
-        weave_c(1,3)
-        quant_h(3,1)
-        mm1(1,0,1)
-        quant_h(3,2)
-        quant_h(3,3)
-        weave_c(1,2)
-        turn_u(3,0)
-        turn_u(3,1)
-        skip(1,0,0)
-        mm1(2,0,0)
-        evac_u(3,0)
-        quant_c(1,1)
-        evac_u(3,1)
-        skip(1,0,1)
-        mm1(2,0,1)
-        weave_y(0,0)
-        quant_c(1,2)
-        skip(2,0,0)
-        mm1(3,0,0)
-        weave_y(1,0)
-        quant_c(1,3)
-        skip(2,0,1)
-        mm1(3,0,1)
-        weave_y(2,0)
-        quant_y(0,0)
-        skip(3,0,0)
-        mm1(0,1,0)
-        quant_y(1,0)
-        skip(3,0,1)
-        sigmoid(0)
-        mm1(0,1,1)
-        skip(0,1,0)
-        quant_y(2,0)
-        sigmoid(1)
-        mm1(1,1,0)
-        skip(0,1,1)
-        weave_y(0,1)
-        mm1(1,1,1)
-        skip(1,1,0)
-        mm2(0,0,0)
-        quant_y(0,1)
-        mm2(0,0,1)
-        skip(1,1,1)
-        weave_y(1,1)
-        finish(0,0)
-        mm2(0,1,0)
-        mm2(0,1,1)
-        mm1(2,1,0)
-        finish(0,1)
-        weave_y(3,0)
-        skip(2,1,0)
-        mm2(1,0,0)
-        mm2(1,0,1)
-        sigmoid(2)
-        mm2(1,1,0)
-        quant_y(1,1)
-        mm2(1,1,1)
-        finish(1,0)
-        mm1(2,1,1)
-        finish(1,1)
-        sigmoid(3)
-        skip(2,1,1)
-        mm2(2,0,0)
-        weave_y(2,1)
-        mm2(2,0,1)
-        mm2(2,1,0)
-        quant_y(3,0)
-        mm2(2,1,1)
-        finish(2,0)
-        mm1(3,1,0)
-        finish(2,1)
-        sigmoid(4)
-        skip(3,1,0)
-        mm2(3,0,0)
-        mm2(3,0,1)
-        sigmoid(5)
-        mm2(3,1,0)
-        quant_y(2,1)
-        mm2(3,1,1)
-        finish(3,0)
-        mm1(3,1,1)
-        finish(3,1)
-        sigmoid(6)
-        skip(3,1,1)
-        mm2(4,0,0)
-        sigmoid(7)
-        mm2(4,0,1)
-        mm2(4,1,0)
-        finish(4,0)
-        mm2(4,1,1)
-        weave_y(3,1)
-        mm2(5,0,0)
-        mm2(5,0,1)
-        finish(4,1)
-        mm2(5,1,0)
-        mm2(5,1,1)
-        quant_y(3,1)
-        finish(5,0)
-        mm2(6,0,0)
-        mm2(6,1,0)
-        finish(5,1)
-        mm2(7,0,0)
-        mm2(7,1,0)
-        mm2(6,0,1)
-        finish(6,0)
-        mm2(6,1,1)
-        mm2(7,0,1)
-        mm2(7,1,1)
-        finish(6,1)
-        finish(7,0)
-        finish(7,1)
+        for q in range(1, GROUPS):
+            load_rows(gate_raw, gate_rows, q, "gate_raw")
+
+        for h in range(HALVES):
+            for q in range(GROUPS):
+                empty_u(q, h)
+            quant_h(h + 1)
+            if h > 0:
+                quant_c(1, 0)
+            weave_c(1, 2 * h)
+            weave_c(1, 2 * h + 1)
+        quant_h(GROUPS - 1)
+        quant_c(1, 1)
+        for q in range(GROUPS):
+            for w in range(2):
+                readout(q, 0, w)
+                add_skip(q, 0, w)
+                if q == 0:
+                    quant_c(1, 2 + w)
+            if q < EARLY_GATES:
+                sigmoid(q)
+            if q < GROUPS - 1:
+                weave_y(q, 0)
+
+        for step in range(TILES + OUT_LAG):
+            q, w = divmod(step, 2)
+            j = step - OUT_LAG
+            if step < TILES:
+                readout(q, 1, w)
+            if j >= 0:
+                project(j)
+            if step < TILES:
+                add_skip(q, 1, w)
+            if 0 <= step - QUANT_LAG < GROUPS * HALVES:
+                quant_y(*divmod(step - QUANT_LAG, HALVES))
+            if j >= 0:
+                finish(j)
+            if step < TILES and w == 1:
+                weave_y(q, 1)
+                if q == 0:
+                    weave_y(GROUPS - 1, 0)
+            if EARLY_GATES <= step - 1 < TILES:
+                sigmoid(step - 1)

@@ -35,6 +35,8 @@ BLOCKS = K // BLK
 WIDEN_ON_SCALAR = (1, 5)
 WEAVE_ON_SCALAR = ((1, 1), (1, 3))
 
+LATE_BLOCKS = 8
+
 OUT_LAG = 4
 QUANT_LAG = 2
 EARLY_GATES = 2
@@ -91,13 +93,14 @@ def tile_state_space_readout_d4_kernel(tc, H_bytes, H_scale, C, u, d, W_words, W
                     in_=W_scales[:, 4 * quad:4 * quad + 4, :].rearrange("h i r -> i h r").bitcast(I32),
                 )
 
-        def widen(j):
-            h_wide[j] = work.tile([P, K], BF16, name="h_wide%d" % j, tag="wide", bufs=TILES)
-            for b in range(BLOCKS):
+        def widen(j, blocks, on_scalar):
+            if blocks.start == 0:
+                h_wide[j] = work.tile([P, K], BF16, name="h_wide%d" % j, tag="wide", bufs=TILES)
+            for b in blocks:
                 cols = slice(b * BLK, (b + 1) * BLK)
                 scale = h_scale[:, j * BLOCKS + b:j * BLOCKS + b + 1]
                 codes = h_raw[j][:, cols].bitcast(FP8)
-                if j in WIDEN_ON_SCALAR:
+                if on_scalar:
                     nc.scalar.activation(out=h_wide[j][:, cols], in_=codes, func=ACT.Copy, scale=scale)
                 else:
                     nc.vector.tensor_scalar(out=h_wide[j][:, cols], in0=codes, scalar1=scale, scalar2=None, op0=ALU.mult)
@@ -111,9 +114,10 @@ def tile_state_space_readout_d4_kernel(tc, H_bytes, H_scale, C, u, d, W_words, W
 
         def turn_h(q, g):
             bank = turn("h_bank%d_%d" % (q, g), lambda i: h_wide[PAIR * q + i][:, g * KP:(g + 1) * KP].bitcast(F32))
-            h_woven[q, g] = work.tile([P, GT * PACK], BF16, name="h_woven%d_%d" % (q, g), tag="h_woven", bufs=12, align_bytes=64)
+            if g == 0:
+                h_woven[q] = work.tile([P, PASSES * GT * PACK], BF16, name="h_woven%d" % q, tag="h_woven", bufs=3, align_bytes=64)
             nc.scalar.copy(
-                out=h_woven[q, g][:].bitcast(F32).rearrange("p (r w) -> p r w", w=2),
+                out=h_woven[q][:].bitcast(F32).rearrange("p (g r w) -> p g r w", g=PASSES, w=2)[:, g, :, :],
                 in_=bank[:].rearrange("p w r -> p r w"),
             )
 
@@ -125,13 +129,12 @@ def tile_state_space_readout_d4_kernel(tc, H_bytes, H_scale, C, u, d, W_words, W
             return code, exp
 
         def quant_h(q):
-            for g in range(PASSES):
-                h_code[q, g], h_exp[q, g] = quantize("h%d_%d" % (q, g), h_woven[q, g])
+            h_code[q], h_exp[q] = quantize("h%d" % q, h_woven[q])
 
         def weave_c(h, g):
             c_woven[h, g] = work.tile([P, KP * PACK], BF16, name="c_woven%d_%d" % (h, g), tag="c_woven", bufs=4, align_bytes=64)
-            dst = c_woven[h, g][:].rearrange("p (t m row) -> p m row t", t=PACK, row=PACK)
-            src = c_raw[h, g][:].rearrange("p row (m t) -> p m row t", t=PACK)
+            dst = c_woven[h, g][:].rearrange("p (t m i row) -> p m t i row", t=PACK, i=2, row=PACK)
+            src = c_raw[h, g][:].rearrange("p row (m i t) -> p m t i row", i=2, t=PACK)
             if (h, g) in WEAVE_ON_SCALAR:
                 nc.scalar.copy(out=dst, in_=src)
             else:
@@ -155,7 +158,7 @@ def tile_state_space_readout_d4_kernel(tc, H_bytes, H_scale, C, u, d, W_words, W
                     nc.tensor.matmul_mx(
                         out=y_bank[q, h, w][:, e, :],
                         lhsT=c_code[h, g][:, cols].bitcast(FP8X4), lhsT_scale=c_exp[h, g][:, cols],
-                        rhs=h_code[q, g][:].bitcast(FP8X4), rhs_scale=h_exp[q, g][:],
+                        rhs=h_code[q][:, g * GT:(g + 1) * GT].bitcast(FP8X4), rhs_scale=h_exp[q][:, g * GT:(g + 1) * GT],
                         start=(g == 0), stop=(g == PASSES - 1),
                     )
 
@@ -215,11 +218,14 @@ def tile_state_space_readout_d4_kernel(tc, H_bytes, H_scale, C, u, d, W_words, W
         nc.sync.dma_start(out=d_col[:], in_=d.rearrange("(h p t) -> p h t", p=P, t=PACK))
         load_c(1, 0)
 
-        for j in range(TILES):
-            widen(j)
+        for j in range(TILES - 1):
+            widen(j, range(BLOCKS), j in WIDEN_ON_SCALAR)
+        widen(TILES - 1, range(BLOCKS - LATE_BLOCKS), False)
         for step in range(GROUPS):
             for g in range(PASSES):
                 turn_h(step, g)
+            if step == 1:
+                widen(TILES - 1, range(BLOCKS - LATE_BLOCKS, BLOCKS), True)
             weave_c(0, step)
             if step + 1 < PASSES:
                 load_c(1, step + 1)
@@ -228,22 +234,23 @@ def tile_state_space_readout_d4_kernel(tc, H_bytes, H_scale, C, u, d, W_words, W
             else:
                 quant_c(0, step - 1)
         quant_c(0, PASSES - 1)
-        for h in range(HALVES):
-            for q in range(GROUPS):
+        for q in range(GROUPS):
+            for h in range(HALVES):
                 turn_u(q, h)
         load_rows(gate_raw, gate_rows, 0, "gate_raw")
         load_w()
         for q in range(1, GROUPS):
             load_rows(gate_raw, gate_rows, q, "gate_raw")
 
-        for h in range(HALVES):
-            for q in range(GROUPS):
-                empty_u(q, h)
-            quant_h(h + 1)
-            if h > 0:
+        for step in range(2):
+            for q in (2 * step, 2 * step + 1):
+                for h in range(HALVES):
+                    empty_u(q, h)
+            quant_h(step + 1)
+            if step > 0:
                 quant_c(1, 0)
-            weave_c(1, 2 * h)
-            weave_c(1, 2 * h + 1)
+            weave_c(1, 2 * step)
+            weave_c(1, 2 * step + 1)
         quant_h(GROUPS - 1)
         quant_c(1, 1)
         for q in range(GROUPS):

@@ -214,7 +214,8 @@ def tile_state_space_readout_d4_kernel(tc, H_bytes, H_scale, C, u, d, W_words, W
             load_h(j)
         for g in range(PASSES):
             load_c(0, g)
-            load_rows(u_raw, u_rows, g, "u_raw")
+        for q in range(GROUPS):
+            load_rows(u_raw, u_rows, q, "u_raw")
         nc.sync.dma_start(out=d_col[:], in_=d.rearrange("(h p t) -> p h t", p=P, t=PACK))
         load_c(1, 0)
 
@@ -242,16 +243,17 @@ def tile_state_space_readout_d4_kernel(tc, H_bytes, H_scale, C, u, d, W_words, W
         for q in range(1, GROUPS):
             load_rows(gate_raw, gate_rows, q, "gate_raw")
 
-        for step in range(2):
-            for q in (2 * step, 2 * step + 1):
-                for h in range(HALVES):
-                    empty_u(q, h)
-            quant_h(step + 1)
-            if step > 0:
-                quant_c(1, 0)
-            weave_c(1, 2 * step)
-            weave_c(1, 2 * step + 1)
-        quant_h(GROUPS - 1)
+        for q in range(GROUPS):
+            for h in range(HALVES):
+                empty_u(q, h)
+        quant_h(1)
+        quant_h(2)
+        weave_c(1, 0)
+        weave_c(1, 1)
+        quant_h(3)
+        quant_c(1, 0)
+        weave_c(1, 2)
+        weave_c(1, 3)
         quant_c(1, 1)
         for q in range(GROUPS):
             for w in range(2):

@@ -37,9 +37,12 @@ WEAVE_ON_SCALAR = ((1, 1), (1, 3))
 
 LATE_BLOCKS = 8
 
+WEAVE_ON_GPSIMD = ((1, 0), (2, 0))
+
 OUT_LAG = 4
 QUANT_LAG = 2
-EARLY_GATES = 2
+LAST_HALF_STEP = 5
+EARLY_GATES = 3
 
 
 def tile_state_space_readout_d4_kernel(tc, H_bytes, H_scale, C, u, d, W_words, W_scales, gate, out):
@@ -175,10 +178,17 @@ def tile_state_space_readout_d4_kernel(tc, H_bytes, H_scale, C, u, d, W_words, W
 
         def weave_y(q, h):
             y_woven[q, h] = work.tile([P, GT * PACK], BF16, name="y_woven%d_%d" % (q, h), tag="y_woven", bufs=6, align_bytes=64)
-            nc.scalar.copy(
-                out=y_woven[q, h][:].rearrange("p (c i t) -> p c t i", i=4, t=PACK),
-                in_=y_planes[q, h][:].rearrange("p t (c i) -> p c t i", i=4),
-            )
+            if (q, h) in WEAVE_ON_GPSIMD:
+                nc.gpsimd.tensor_scalar(
+                    out=y_woven[q, h][:].rearrange("p (r t) -> p r t", t=PACK),
+                    in0=y_planes[q, h][:].rearrange("p t r -> p r t"),
+                    scalar1=1.0, scalar2=0.0, op0=ALU.mult, op1=ALU.add,
+                )
+            else:
+                nc.scalar.copy(
+                    out=y_woven[q, h][:].rearrange("p (c i t) -> p c t i", i=4, t=PACK),
+                    in_=y_planes[q, h][:].rearrange("p t (c i) -> p c t i", i=4),
+                )
 
         def quant_y(q, h):
             y_code[q, h], y_exp[q, h] = quantize("y%d_%d" % (q, h), y_woven[q, h])
@@ -203,11 +213,10 @@ def tile_state_space_readout_d4_kernel(tc, H_bytes, H_scale, C, u, d, W_words, W
                         start=(h == 0), stop=(h == HALVES - 1),
                     )
 
-        def finish(j):
-            for s in range(SPANS):
-                part = gated[j][:, BANK * s:BANK * (s + 1)]
-                nc.vector.tensor_tensor(out=part, in0=out_bank[j, s][:], in1=part, op=ALU.mult)
-                nc.sync.dma_start(out=out_rows[:, j, BANK * s:BANK * (s + 1)], in_=part)
+        def finish(j, s):
+            part = gated[j][:, BANK * s:BANK * (s + 1)]
+            nc.vector.tensor_tensor(out=part, in0=out_bank[j, s][:], in1=part, op=ALU.mult)
+            nc.sync.dma_start(out=out_rows[:, j, BANK * s:BANK * (s + 1)], in_=part)
 
         nc.sync.dma_start(out=h_scale[:], in_=H_scale.rearrange("(p j) b -> p (j b)", j=TILES))
         for j in range(TILES):
@@ -275,10 +284,15 @@ def tile_state_space_readout_d4_kernel(tc, H_bytes, H_scale, C, u, d, W_words, W
                 project(j)
             if step < TILES:
                 add_skip(q, 1, w)
-            if 0 <= step - QUANT_LAG < GROUPS * HALVES:
+            if 0 <= step - QUANT_LAG < (GROUPS - 1) * HALVES:
                 quant_y(*divmod(step - QUANT_LAG, HALVES))
+            if step == LAST_HALF_STEP:
+                quant_y(GROUPS - 1, 0)
             if j >= 0:
-                finish(j)
+                finish(j, 0)
+                if step == TILES:
+                    quant_y(GROUPS - 1, 1)
+                finish(j, 1)
             if step < TILES and w == 1:
                 weave_y(q, 1)
                 if q == 0:

from contextlib import ExitStack

import concourse.mybir as mybir
from concourse.masks import make_identity

T, K, N, R = 1024, 2048, 1024, 1024
FLOPS = 2 * T * K * N + 2 * T * N * R

F32 = mybir.dt.float32
BF16 = mybir.dt.bfloat16
U32 = mybir.dt.uint32
I32 = mybir.dt.int32
U8 = mybir.dt.uint8
FP8 = mybir.dt.float8_e4m3fn
FP8X4 = mybir.dt.float8_e4m3fn_x4
FP4X4 = mybir.dt.float4_e2m1fn_x4
ALU = mybir.AluOpType
ACT = mybir.ActivationFunctionType

P = 128
PACK = 4
KP = P * PACK
WORDS = KP // 2
TILES = T // P
PAIR = 2
GT = PAIR * P
GROUPS = TILES // PAIR
PASSES = K // KP
HALVES = N // KP
BANK = 512
SPANS = R // BANK
BLK = 128
BLOCKS = K // BLK

WIDEN_ON_SCALAR = (1, 5)
WEAVE_ON_SCALAR = ((1, 1), (1, 3))

LATE_BLOCKS = 8

WEAVE_ON_GPSIMD = ((1, 0), (2, 0))

OUT_LAG = 4
QUANT_LAG = 2
LAST_HALF_STEP = 5
EARLY_GATES = 3


def tile_state_space_readout_d4_kernel(tc, H_bytes, H_scale, C, u, d, W_words, W_scales, gate, out):
    nc = tc.nc
    with ExitStack() as ctx:
        keep = ctx.enter_context(tc.tile_pool(name="keep", bufs=1))
        work = ctx.enter_context(tc.tile_pool(name="work", bufs=2))
        psum = ctx.enter_context(tc.psum_pool(name="psum", bufs=8))
        ctx.enter_context(tc.manual_schedule())

        h_rows = H_bytes.rearrange("(p j) k -> p j k", j=TILES)
        u_rows = u.rearrange("(p j) n -> p (j n)", j=TILES)
        gate_rows = gate.rearrange("(p j) r -> p (j r)", j=TILES)
        out_rows = out.rearrange("(p j) r -> p j r", j=TILES)

        ident = keep.tile([P, P], F32, name="ident")
        w_scale = keep.tile([P, HALVES, R], U8, name="w_scale", align_bytes=64)
        table_probe = keep.tile([P, 2], F32, name="table_probe")
        make_identity(nc, ident[:])
        nc.scalar.activation(out=table_probe[:], in_=ident[:, 0:2], func=ACT.Sigmoid)
        nc.gpsimd.memset(w_scale[:].rearrange("p h r -> p (h r)").bitcast(I32), 0)

        h_scale = keep.tile([P, TILES * BLOCKS], F32, name="h_scale")
        d_col = keep.tile([P, HALVES, PACK], BF16, name="d_col")
        w_words = keep.tile([P, HALVES, 2 * R], U8, name="w_words", align_bytes=64)
        h_raw, c_raw, u_raw, gate_raw = {}, {}, {}, {}
        h_wide, h_woven, h_code, h_exp = {}, {}, {}, {}
        c_woven, c_code, c_exp = {}, {}, {}
        u_bank, u_turned = {}, {}
        y_bank, y_planes, y_woven, y_code, y_exp = {}, {}, {}, {}, {}
        gated, out_bank = {}, {}

        def load_h(j):
            h_raw[j] = keep.tile([P, K], U8, name="h_raw%d" % j)
            nc.sync.dma_start(out=h_raw[j][:], in_=h_rows[:, j, :])

        def load_c(h, g):
            c_raw[h, g] = work.tile([P, PACK, KP], BF16, name="c_raw%d_%d" % (h, g), tag="c_raw", bufs=5)
            rows = C[g * KP:(g + 1) * KP, h * KP:(h + 1) * KP]
            nc.sync.dma_start(out=c_raw[h, g][:], in_=rows.rearrange("(p t) n -> p t n", t=PACK))

        def load_rows(tiles, rows, q, label):
            tiles[q] = work.tile([P, PAIR * N], BF16, name="%s%d" % (label, q), tag="rows", bufs=5)
            nc.sync.dma_start(out=tiles[q][:], in_=rows[:, q * PAIR * N:(q + 1) * PAIR * N])

        def load_w():
            nc.sync.dma_start(out=w_words[:], in_=W_words.rearrange("h p b -> p h b"))
            for quad in range(4):
                nc.sync.dma_start(
                    out=w_scale[32 * quad:32 * quad + 4, :, :].bitcast(I32),
                    in_=W_scales[:, 4 * quad:4 * quad + 4, :].rearrange("h i r -> i h r").bitcast(I32),
                )

        def widen(j, blocks, on_scalar):
            if blocks.start == 0:
                h_wide[j] = work.tile([P, K], BF16, name="h_wide%d" % j, tag="wide", bufs=TILES)
            for b in blocks:
                cols = slice(b * BLK, (b + 1) * BLK)
                scale = h_scale[:, j * BLOCKS + b:j * BLOCKS + b + 1]
                codes = h_raw[j][:, cols].bitcast(FP8)
                if on_scalar:
                    nc.scalar.activation(out=h_wide[j][:, cols], in_=codes, func=ACT.Copy, scale=scale)
                else:
                    nc.vector.tensor_scalar(out=h_wide[j][:, cols], in0=codes, scalar1=scale, scalar2=None, op0=ALU.mult)

        def turn(name, words_of_tile):
            bank = psum.tile([P, 2, GT], F32, name=name, tag="bank")
            for i in range(PAIR):
                for w in range(2):
                    nc.tensor.transpose(bank[:, w, i * P:(i + 1) * P], words_of_tile(i)[:, w:WORDS:2], ident[:])
            return bank

        def turn_h(q, g):
            bank = turn("h_bank%d_%d" % (q, g), lambda i: h_wide[PAIR * q + i][:, g * KP:(g + 1) * KP].bitcast(F32))
            if g == 0:
                h_woven[q] = work.tile([P, PASSES * GT * PACK], BF16, name="h_woven%d" % q, tag="h_woven", bufs=3, align_bytes=64)
            nc.scalar.copy(
                out=h_woven[q][:].bitcast(F32).rearrange("p (g r w) -> p g r w", g=PASSES, w=2)[:, g, :, :],
                in_=bank[:].rearrange("p w r -> p r w"),
            )

        def quantize(name, woven):
            columns = woven[:].shape[1] // PACK
            code = keep.tile([P, columns], U32, name=name + "_code", align_bytes=64)
            exp = keep.tile([P, columns], U8, name=name + "_exp", align_bytes=64)
            nc.vector.quantize_mx(out=code[:].bitcast(FP8X4), scales=exp[:], in_=woven[:])
            return code, exp

        def quant_h(q):
            h_code[q], h_exp[q] = quantize("h%d" % q, h_woven[q])

        def weave_c(h, g):
            c_woven[h, g] = work.tile([P, KP * PACK], BF16, name="c_woven%d_%d" % (h, g), tag="c_woven", bufs=4, align_bytes=64)
            dst = c_woven[h, g][:].rearrange("p (t m i row) -> p m t i row", t=PACK, i=2, row=PACK)
            src = c_raw[h, g][:].rearrange("p row (m i t) -> p m t i row", i=2, t=PACK)
            if (h, g) in WEAVE_ON_SCALAR:
                nc.scalar.copy(out=dst, in_=src)
            else:
                nc.vector.tensor_copy(out=dst, in_=src)

        def quant_c(h, g):
            c_code[h, g], c_exp[h, g] = quantize("c%d_%d" % (h, g), c_woven[h, g])

        def turn_u(q, h):
            u_bank[q, h] = turn("u_bank%d_%d" % (q, h), lambda i: u_raw[q][:, i * N + h * KP:i * N + (h + 1) * KP].bitcast(F32))

        def empty_u(q, h):
            u_turned[q, h] = keep.tile([P, 2 * GT], F32, name="u_turned%d_%d" % (q, h))
            nc.scalar.copy(out=u_turned[q, h][:], in_=u_bank[q, h][:].rearrange("p w r -> p (w r)"))

        def readout(q, h, w):
            y_bank[q, h, w] = psum.tile([P, 2, GT], F32, name="y_bank%d_%d_%d" % (q, h, w), tag="bank")
            for e in range(2):
                cols = slice((2 * w + e) * P, (2 * w + e + 1) * P)
                for g in range(PASSES):
                    nc.tensor.matmul_mx(
                        out=y_bank[q, h, w][:, e, :],
                        lhsT=c_code[h, g][:, cols].bitcast(FP8X4), lhsT_scale=c_exp[h, g][:, cols],
                        rhs=h_code[q][:, g * GT:(g + 1) * GT].bitcast(FP8X4), rhs_scale=h_exp[q][:, g * GT:(g + 1) * GT],
                        start=(g == 0), stop=(g == PASSES - 1),
                    )

        def add_skip(q, h, w):
            if w == 0:
                y_planes[q, h] = work.tile([P, PACK, GT], BF16, name="y_planes%d_%d" % (q, h), tag="y_planes", bufs=6)
            u_planes = u_turned[q, h][:].bitcast(BF16).rearrange("p (w r e) -> p w e r", w=2, e=2)
            for e in range(2):
                t = 2 * w + e
                nc.vector.scalar_tensor_tensor(
                    out=y_planes[q, h][:, t, :], in0=u_planes[:, w, e, :], scalar=d_col[:, h, t:t + 1],
                    in1=y_bank[q, h, w][:, e, :], op0=ALU.mult, op1=ALU.add,
                )

        def weave_y(q, h):
            y_woven[q, h] = work.tile([P, GT * PACK], BF16, name="y_woven%d_%d" % (q, h), tag="y_woven", bufs=6, align_bytes=64)
            if (q, h) in WEAVE_ON_GPSIMD:
                nc.gpsimd.tensor_scalar(
                    out=y_woven[q, h][:].rearrange("p (r t) -> p r t", t=PACK),
                    in0=y_planes[q, h][:].rearrange("p t r -> p r t"),
                    scalar1=1.0, scalar2=0.0, op0=ALU.mult, op1=ALU.add,
                )
            else:
                nc.scalar.copy(
                    out=y_woven[q, h][:].rearrange("p (c i t) -> p c t i", i=4, t=PACK),
                    in_=y_planes[q, h][:].rearrange("p t (c i) -> p c t i", i=4),
                )

        def quant_y(q, h):
            y_code[q, h], y_exp[q, h] = quantize("y%d_%d" % (q, h), y_woven[q, h])

        def sigmoid(j):
            gated[j] = work.tile([P, R], F32, name="gated%d" % j, tag="wide", bufs=TILES)
            q, i = divmod(j, PAIR)
            nc.scalar.activation(out=gated[j][:], in_=gate_raw[q][:, i * R:(i + 1) * R], func=ACT.Sigmoid)

        def project(j):
            q, i = divmod(j, PAIR)
            tokens = slice(i * P, (i + 1) * P)
            for h in range(HALVES):
                for s in range(SPANS):
                    if h == 0:
                        out_bank[j, s] = psum.tile([P, BANK], F32, name="out_bank%d_%d" % (j, s), tag="bank")
                    nc.tensor.matmul_mx(
                        out=out_bank[j, s][:],
                        lhsT=y_code[q, h][:, tokens].bitcast(FP8X4), lhsT_scale=y_exp[q, h][:, tokens],
                        rhs=w_words[:, h, 2 * BANK * s:2 * BANK * (s + 1)].bitcast(FP4X4),
                        rhs_scale=w_scale[:, h, BANK * s:BANK * (s + 1)],
                        start=(h == 0), stop=(h == HALVES - 1),
                    )

        def finish(j, s):
            part = gated[j][:, BANK * s:BANK * (s + 1)]
            nc.vector.tensor_tensor(out=part, in0=out_bank[j, s][:], in1=part, op=ALU.mult)
            nc.sync.dma_start(out=out_rows[:, j, BANK * s:BANK * (s + 1)], in_=part)

        nc.sync.dma_start(out=h_scale[:], in_=H_scale.rearrange("(p j) b -> p (j b)", j=TILES))
        for j in range(TILES):
            load_h(j)
        for g in range(PASSES):
            load_c(0, g)
        for q in range(GROUPS):
            load_rows(u_raw, u_rows, q, "u_raw")
        nc.sync.dma_start(out=d_col[:], in_=d.rearrange("(h p t) -> p h t", p=P, t=PACK))
        load_c(1, 0)

        for j in range(TILES - 1):
            widen(j, range(BLOCKS), j in WIDEN_ON_SCALAR)
        widen(TILES - 1, range(BLOCKS - LATE_BLOCKS), False)
        for step in range(GROUPS):
            for g in range(PASSES):
                turn_h(step, g)
            if step == 1:
                widen(TILES - 1, range(BLOCKS - LATE_BLOCKS, BLOCKS), True)
            weave_c(0, step)
            if step + 1 < PASSES:
                load_c(1, step + 1)
            if step == 0:
                quant_h(0)
            else:
                quant_c(0, step - 1)
        quant_c(0, PASSES - 1)
        for q in range(GROUPS):
            for h in range(HALVES):
                turn_u(q, h)
        load_rows(gate_raw, gate_rows, 0, "gate_raw")
        load_w()
        for q in range(1, GROUPS):
            load_rows(gate_raw, gate_rows, q, "gate_raw")

        for q in range(GROUPS):
            for h in range(HALVES):
                empty_u(q, h)
        quant_h(1)
        quant_h(2)
        weave_c(1, 0)
        weave_c(1, 1)
        quant_h(3)
        quant_c(1, 0)
        weave_c(1, 2)
        weave_c(1, 3)
        quant_c(1, 1)
        for q in range(GROUPS):
            for w in range(2):
                readout(q, 0, w)
                add_skip(q, 0, w)
                if q == 0:
                    quant_c(1, 2 + w)
            if q < EARLY_GATES:
                sigmoid(q)
            if q < GROUPS - 1:
                weave_y(q, 0)

        for step in range(TILES + OUT_LAG):
            q, w = divmod(step, 2)
            j = step - OUT_LAG
            if step < TILES:
                readout(q, 1, w)
            if j >= 0:
                project(j)
            if step < TILES:
                add_skip(q, 1, w)
            if 0 <= step - QUANT_LAG < (GROUPS - 1) * HALVES:
                quant_y(*divmod(step - QUANT_LAG, HALVES))
            if step == LAST_HALF_STEP:
                quant_y(GROUPS - 1, 0)
            if j >= 0:
                finish(j, 0)
                if step == TILES:
                    quant_y(GROUPS - 1, 1)
                finish(j, 1)
            if step < TILES and w == 1:
                weave_y(q, 1)
                if q == 0:
                    weave_y(GROUPS - 1, 0)
            if EARLY_GATES <= step - 1 < TILES:
                sigmoid(step - 1)
